import numpy as np, ml_dtypes
CORES = [9,25,41,57]
N = 4
import mx_ref
BF = ml_dtypes.bfloat16
def pick(q, e):
    c = np.concatenate([q[0].reshape(128, -1, 4), np.zeros((128, 1, 4), np.uint8)], axis=1); s = np.concatenate([q[1], np.ones((16, 1), np.uint8)], axis=1)
    return (np.ascontiguousarray(c[:, e].reshape(128, -1)), np.ascontiguousarray(s[:, e]))
def join(*qs):
    return (np.concatenate([q[0] for q in qs], axis=1), np.concatenate([q[1] for q in qs], axis=1))
def put(q, e, v):
    c, s = q[0].reshape(128, -1, 4).copy(), q[1].copy(); c[:, e] = v[0].reshape(128, -1, 4); s[:, e] = v[1]
    return (c.reshape(128, -1), s)
def pk(c, s):
    return (np.ascontiguousarray(c), mx_ref.live(s))
def emit(q):
    return q[0], q[1]
def decode(q):
    o = []
    for b in range(4):
        e = np.zeros((128, 128, 4), np.float32); e[np.arange(128), np.arange(128), b] = 1
        o.append(mx_ref.matmul(mx_ref.quantize(e.reshape(128, 512).astype(BF)), q))
    return np.stack(o, axis=2).reshape(128, -1)
def cut(t, i, w=512):
    return t[:, w * i:w * i + w]
def f(rng, *shape):
    return mx_ref.flush((rng.standard_normal(shape, dtype=np.float32) * np.exp2(rng.integers(-2, 3, shape[:-1] + (1,)))).astype(BF))
def wide(rng, *shape, cols=0):
    v = rng.standard_normal(shape, dtype=np.float32) * np.exp2(rng.integers(-12, 13, shape)).astype(np.float32)
    if cols: v *= np.repeat(np.exp2(rng.integers(-cols, cols + 1, shape[:-2] + (1, shape[-1] // 4))) * (rng.random(shape[:-2] + (1, shape[-1] // 4)) > 0.0625), 4, axis=-1).astype(np.float32)
    return mx_ref.flush(v.astype(BF))
P, K, O, L = 512, 192, 2, 2
def times(t, v):
    v = t.astype(np.float32) * np.asarray(v, np.float32)
    return np.where(np.abs(v) < 2.0 ** -16, 0, v).astype(np.float32).astype(BF)
def loud(u, e):
    v = u.astype(np.float32) * np.float32(2.0 ** e)
    return np.where(np.abs(v) < 2.0 ** -30, 0, v).astype(np.float32).astype(BF)
def strong(rng, u, n):
    return np.sign(u[0, :, None, :4].astype(np.float32)) * (1 + rng.random((128, n, 4))) * 128
def near(rng, u):
    ku, v = mx_ref.quantize(np.ascontiguousarray(u[0])), np.repeat(strong(rng, u, 1), 12, axis=1).astype(np.float32)
    v[127] = 0
    z = size(ku, mx_ref.quantize(np.ascontiguousarray(v.reshape(128, -1).astype(BF))))
    v[127, 1:, 0] = np.exp2(np.floor(np.log2(z[0])) - 23 + np.arange(11))
    z = size(ku, mx_ref.quantize(np.ascontiguousarray(v.reshape(128, -1).astype(BF))))
    return v[:, [0, int(np.argmax(z > z[0]))]]
def plain(rng):
    k = np.exp2(6 * rng.random(P) - 3) * np.exp2(rng.random((N, P)) - 0.5)
    u = np.zeros((N, 128, 512), BF)
    u[:, :, :4] = f(rng, 128, 4)
    return {"gr": times(f(rng, N, 128, 4 * P), np.repeat(k, 4, axis=1)[:, None]), "u": u, "w": f(rng, N, 128, 512 * O)}
def setup_inputs(rng):
    return plain(rng)
def setup_inputs_apart(rng):
    d, h = plain(rng), K // 2
    d["u"][:, :8] = 0
    d["u"][:, 120:] = 0
    d["u"][:, 127, 0] = 1
    g = d["gr"].astype(np.float32).reshape(N, 128, P, 4) * np.float32(2.0 ** -8)
    x = rng.permutation(P)[:N // 2 * K].reshape(N // 2, 2, h)
    c = near(rng, d["u"])
    for j in range(N // 2):
        rest = rng.permutation(np.setdiff1d(np.arange(P), x[j].reshape(-1)))[:K].reshape(2, h)
        for i in range(2):
            v = c[:, (x[j, i] >= P // 2).astype(int)]
            v[:8] = (1 + rng.random((8, h, 4))) * 128 * rng.choice([-1.0, 1.0], (8, h, 4))
            g[2 * j + i][:, x[j, i]] = v * np.exp2(rng.integers(0, 3, h))[:, None]
            g[2 * j + i][:, rest[i]] = strong(rng, d["u"], h) * 2.0 ** -4
    d["gr"] = times(g.reshape(N, 128, -1), 1)
    return d
def setup_inputs_cancel(rng):
    d, m = plain(rng), K // 8
    g = d["gr"].astype(np.float32).reshape(N, 128, P, 4)
    e = rng.permutation(P)[:3 * L * m].reshape(L, 3, m)
    g[:, :, e.reshape(-1)] = 0
    for b in range(L):
        for r in range(N):
            h = (r >> b) & 1
            g[r][:, e[b, 1 + h]] = strong(rng, d["u"], m)
            if r % (1 << b) == 0:
                g[r][:, e[b, 0]] = -g[r - (1 << b)][:, e[b, 0]] if h else strong(rng, d["u"], m)
    d["gr"] = times(g.reshape(N, 128, -1), 2.0 ** -10)
    d["u"] = loud(d["u"], -26)
    return d
def setup_inputs_few(rng):
    d, m, h = plain(rng), K // 8, N // 2
    d["u"][:, :64] = 0
    g = d["gr"].astype(np.float32).reshape(N, 128, P, 4)
    g[:, 64:] = 0
    g *= (np.arange(P) % 4 != rng.integers(0, 4, (N, 1)))[:, None, :, None]
    low, e = rng.permutation(K // 4)[:m], K + rng.permutation(P - K)[:(h + 3) * m].reshape(h + 3, m)
    c = np.concatenate([low, e[0]])
    for r in range(N):
        own = e[3 + r] if r < h else e[1:3].reshape(-1)
        g[r][:, own] += strong(rng, d["u"], own.size)
        if r % 2: g[r][:, c] = -g[r - 1][:, c]
        else: g[r][:, c] += strong(rng, d["u"], c.size)
    d["gr"] = times(g.reshape(N, 128, -1), 1)
    d["u"] = loud(d["u"], 24)
    return d
def setup_inputs_spread(rng):
    d = plain(rng)
    e = rng.permutation(P)[:K]
    k = np.exp2(rng.integers(-12, -5, (N, P))) * (rng.random((N, P)) > 0.0625)
    k[:, e] = np.exp2(rng.integers(0, 7, (N, K))) * rng.choice([-1.0, 1.0], (N, K))
    g = wide(rng, N, 128, 4 * P).astype(np.float32).reshape(N, 128, P, 4)
    g[:, :, e] = np.abs(g[:, :, e]) * np.sign(d["u"][0, :, None, :4].astype(np.float32))
    d["gr"] = times(g.reshape(N, 128, -1), np.repeat(k, 4, axis=1)[:, None])
    return d
def setup_inputs_ties(rng):
    d = plain(rng)
    x = f(rng, 128, 24).astype(np.float32).reshape(128, 6, 4)
    h = np.stack([rng.permutation(P) % 6 for r in range(N)])
    sign = rng.choice([-1.0, 1.0], (N, 1, P, 1))
    d["gr"] = times((np.moveaxis(x[:, h], 1, 0) * sign).reshape(N, 128, -1), 1)
    return d
def check_inputs(d):
    b = []
    for k, lo, hi in (("gr", -16, 24), ("u", -30, 30), ("w", -30, 30)):
        v = np.abs(d[k].astype(np.float32))
        if not (np.isfinite(v).all() and ((v == 0) | (v >= 2.0 ** lo) & (v <= 2.0 ** hi)).all()): b.append("a value of " + k)
    v = d["u"].astype(np.float32)
    if (v[:, :, 4:] != 0).any(): b.append("u has numbers behind its column 0")
    if (v != v[:1]).any(): b.append("u isn't the same on all ranks")
    return b
def size(ku, q):
    return np.abs(mx_ref.matmul(ku, q)[0])
def best(s):
    return np.sort(np.argsort(-s, kind="stable")[:K])
def merge(ku, a, b):
    i, j = np.intersect1d(a[0], b[0], return_indices=True)[1:]
    q = join(a[1], b[1])
    v = decode(q).reshape(128, 2 * K, 4)
    v[:, i] = v[:, i] + v[:, K + j]
    q = put(q, i, pick(mx_ref.quantize(np.ascontiguousarray(v.reshape(128, -1).astype(BF))), i))
    n = np.concatenate([a[0], b[0]])
    e = np.setdiff1d(np.arange(2 * K), K + j)
    e = e[np.argsort(n[e])]
    e = e[best(size(ku, q)[e])]
    return n[e], pick(q, e)
def reference(gr, u, w):
    ku, S = [mx_ref.quantize(np.ascontiguousarray(u[r])) for r in range(N)], []
    for r in range(N):
        q = mx_ref.quantize(np.ascontiguousarray(gr[r]))
        e = best(size(ku[r], q))
        S.append((e, pick(q, e)))
    for b in range(L):
        new = list(S)
        for r in range(N):
            p = r ^ (1 << b)
            if r < p: new[r] = new[p] = merge(ku[r], S[r], S[p])
        S = new
    oc, osc = np.zeros((N, 128, 4 * K), np.uint8), np.zeros((N, 16, K), np.uint8)
    nb, y = np.zeros((N, 1, K), np.float32), np.zeros((N, 128, O * K), np.float32)
    for r in range(N):
        oc[r], osc[r] = emit(S[r][1])
        nb[r, 0] = S[r][0]
        for o in range(O): y[r, :, o * K:o * K + K] = mx_ref.matmul(mx_ref.quantize(np.ascontiguousarray(cut(w[r], o))), S[r][1])
    return {"oc": oc, "osc": osc, "nb": nb, "y": y}

@@ -1,0 +1,700 @@
+from concourse.mybir import dt, AluOpType as OP, ActivationFunctionType as AF
+
+P, K, O = 512, 192, 2
+WA, WB, WZ, WM, WY, WE = 32, 224, 416, 448, 640, 704
+NSEM = 48
+MID = 352
+ROUND16 = 1.5 * 2.0 ** 27
+BF, F32, I32, U16, CODE, U8 = "bfloat16", "float32", "int32", "uint16", "float8_e4m3fn_x4", "uint8"
+SCRATCH = {"ps": ("psum", [128, 4096], F32)}
+PLACE = {}
+_TOP = {}
+_ALIGN = {BF: 16, F32: 8, I32: 8, U16: 16}
+_ALONE = ("ut", "urt", "grt", "wt", "nbw", "yb")
+_CONST = []
+ORDER = {}
+TRIALS, MOVES = 60, 24000
+GUESSES = ((1.0, 1.0, 100.0, 0.0, 1500.0, 1700.0), (1.2, 1.2, 60.0, 20.0, 2000.0, 2500.0), (1.0, 0.8, 200.0, 50.0, 1500.0, 2000.0), (1.3, 1.6, 100.0, 50.0, 1500.0, 2000.0))
+BASE = (29700.0, 35200.0, 34000.0, 40900.0)
+
+
+def _buf(name, n, t):
+    assert name not in PLACE, name
+    if t in _ALIGN and name not in _ALONE:
+        home = ("k" if name in _CONST else "m") + t
+        top = _TOP.get(home, 0)
+        PLACE[name] = (home, top, n)
+        _TOP[home] = -(-(top + n) // _ALIGN[t]) * _ALIGN[t]
+        SCRATCH[home] = ("sbuf", [128, _TOP[home]], t)
+    else:
+        SCRATCH[name] = ("sbuf", [128, n], t)
+        PLACE[name] = (name, 0, n)
+
+
+def _mx(name, n):
+    _buf(name, n, CODE)
+    _buf(name + "s", n, U8)
+
+
+for _n, _w, _t in (
+        ("one", 512, BF), ("zt", 544, BF), ("i16", K, BF), ("i192", K, BF), ("idt", 128, BF), ("ebf", 528, BF), ("e2t", 512, BF), ("mone", 128, BF), ("tri0", 128, BF),
+        ("ni", 1, I32), ("nl", 1, I32), ("nf", 4, F32), ("nlf", 1, F32), ("nx", 4, F32), ("nrept", 1088, BF), ("dlt", 512, BF), ("trit", 1024, BF),
+        ("jx", 2, F32), ("jdt", 512, BF), ("idn", 4 * K, BF), ("zo", 8, U16),
+        ("kw", 12, F32), ("jw", 3, I32), ("jf", 3, F32), ("jwf", 3, F32), ("dl", 3, F32), ("dh0", 3, F32),
+        ("isa", 3, F32), ("nisa", 3, F32), ("basea", 3, F32), ("b511", 4, F32),
+        ("lk", K, F32), ("cn", 1, F32), ("cw", 1, F32), ("cz", 1, F32), ("cth", 1, F32)):
+    _CONST.append(_n)
+    _buf(_n, _w, _t)
+for _n, _w, _t in (
+        ("ut", 4, BF), ("urt", 552, BF), ("grt", 4 * P, BF), ("wt", 1024, BF),
+        ("srow", P, F32), ("scol", 4, F32), ("xd", 512, BF), ("c0t", 4 * P, BF), ("p0", 16, F32), ("junk", 10 * 128, BF), ("junk2", 4 * K, BF), ("junk3", 4 * K, BF),
+        ("x0", 4, F32), ("x1", 4, F32), ("x2", 4, F32), ("x3", 4, F32), ("rk0", 4, F32), ("ot", 4 * K, BF), ("sc", K, F32), ("off0", 12, U16),
+        ("ordt", 4 * 384, BF), ("nnc", 3, F32), ("misc", 832, BF), ("dht", 512, BF), ("tau", 4 * K, BF), ("ct", 4 * K, BF), ("st", 4 * K, BF),
+        ("ntk", 3, F32), ("ntk2", 3, F32), ("plc", 3, F32), ("nbw", K, F32), ("yb", O * K, F32)):
+    _buf(_n, _w, _t)
+for _n, _w in (("ur", 128), ("uq", 136), ("q0", P), ("wq", 256), ("oneq", 128), ("zq", 128), ("nrep", 256), ("dlq", 128), ("eq", 640), ("triq", 256),
+               ("jdq", 128), ("idq", K), ("ndcq", 144), ("c0q", P), ("oh", 320), ("ordq", 384), ("xq", 128), ("rep", 128), ("repb", 128), ("fin", K)):
+    _mx(_n, _w)
+for _s in "01":
+    for _n, _w, _t in (
+            ("na", 3, F32), ("nc", 3, F32), ("nr", 384, BF), ("mt", 4 * K, BF), ("scb", K, F32), ("off1", 12, U16), ("offb", 12, U16), ("ub", 12, F32), ("ub2", 12, F32),
+            ("bor", K, BF), ("keep", 2, F32), ("fm", 2, F32), ("dhr", 2, F32), ("du", 2, F32), ("fo", 3, F32), ("bi", 2, F32),
+            ("ht", 4 * K, BF), ("arow", K, F32), ("acol", 3, F32), ("v", 3 * K, BF), ("rs", 3, F32), ("bs", 3, F32), ("rf", 3, F32),
+            ("scs", K, F32), ("offs", 12, U16)):
+        _buf(_n + _s, _w, _t)
+    for _n, _w in (("nbq", 128), ("tl", 128), ("mtq", 256), ("win", WE), ("an", K), ("bp", K), ("ftq", 136), ("dhq", 128), ("tauq", K), ("ndq", 136), ("cq", 256), ("sq", 320)):
+        _mx(_n + _s, _w)
+ARR = ["tc0", "ts0", "wc0", "ws0", "tc1", "ts1", "wc1", "ws1"]
+SEMAPHORES = ["q_v", "q_s", "q_t", "q_g"] + ["d%d" % i for i in range(NSEM)] + ["l_" + a for a in ARR] + ["a_" + a for a in ARR]
+
+
+def rank_program(g, core, T, topo):
+    rank = T.rank_of(core)
+    if rank is None:
+        return
+    ENG = {"v": g.vector, "s": g.scalar, "t": g.tensor, "g": g, "y": g.sync}
+    prog, nd, sent = [], [0], {}
+
+    def v(name, a=0, b=None, s=1, p=0, e=128, cast=None):
+        if name == "ps":
+            return (name, a, b, s, p, e, cast)
+        home, o, n = PLACE[name]
+        return (home, o + a, o + (n if b is None else b), s, p, e, cast)
+
+    def ap(x):
+        if not isinstance(x, tuple):
+            return x
+        name, a, b, s, p, e, cast = x
+        t = T[name]
+        r = t[p:e, a:b] if s == 1 else t[p:e, a:b:s]
+        if cast is None:
+            return r
+        return r.bitcast(dt.uint8 if cast == 8 else dt.uint32)
+
+    def width(x):
+        return len(range(x[1], x[2], x[3]))
+
+    def overlap(x, y):
+        if x[0] == "ps":
+            f = lambda r: set(c // 512 for c in range(r[1], r[2], r[3] if r[3] == 512 else 1))
+            return bool(f(x) & f(y))
+        if x[1] >= y[2] or y[1] >= x[2]:
+            return False
+        if x[3] == y[3] and x[3] > 1:
+            return (x[1] - y[1]) % x[3] == 0
+        return True
+
+    def rec(q, fn, reads, writes, cost, kind="c", sem=None, amount=0, after=()):
+        prog.append({"q": q, "fn": fn, "reads": reads, "writes": writes, "cost": cost, "kind": kind, "sem": sem, "amount": amount, "after": list(after)})
+        return len(prog) - 1
+
+    tens = lambda *xs: [x for x in xs if isinstance(x, tuple)]
+    short = lambda x: x[0][1:] in (BF, U16) or x[0] in ("ut", "urt", "grt", "wt")
+
+    def easy(*xs):
+        return 0.83 * max(64, width(xs[0]) * (0.5 if all(short(x) for x in xs) else 1))
+
+    def ts(out, in0, s1, op0, s2=None, op1=None):
+        if op1 is None:
+            fn = lambda: g.vector.tensor_scalar(out=ap(out), in0=ap(in0), scalar1=ap(s1), scalar2=None, op0=op0)
+        else:
+            fn = lambda: g.vector.tensor_scalar(out=ap(out), in0=ap(in0), scalar1=ap(s1), scalar2=ap(s2), op0=op0, op1=op1)
+        return rec("v", fn, tens(in0, s1, s2), [out], easy(out, in0))
+
+    def tt(out, a, b, op):
+        f = 1 if "ps" in (a[0], b[0]) else 2
+        rec("v", lambda: g.vector.tensor_tensor(out=ap(out), in0=ap(a), in1=ap(b), op=op), [a, b], [out], 0.83 * max(64, f * width(out)))
+
+    def cp(out, a):
+        rec("v", lambda: g.vector.tensor_copy(ap(out), ap(a)), [a], [out], easy(out, a))
+
+    def fill(out, c=0.0):
+        rec("v", lambda: g.vector.memset(ap(out), c), [], [out], easy(out))
+
+    def act(out, a, func, bias=None, scale=None, accum=None):
+        kw = {}
+        if bias is not None:
+            kw["bias"] = bias
+        if scale is not None:
+            kw["scale"] = scale
+        if accum is not None:
+            kw["accum_out"] = accum
+        rec("s", lambda: g.scalar.activation(ap(out), ap(a), func, **{k: ap(x) for k, x in kw.items()}), tens(a, bias, scale), tens(out, accum), 0.83 * max(64, width(out)) + (20 if accum else 0))
+
+    def zero(out):
+        act(out, v("zt", 0, width(out)), AF.Copy)
+
+    def pl(x):
+        return (x[0] + "s",) + x[1:6] + (None,)
+
+    def quant(out, a):
+        return rec("v", lambda: g.vector.quantize_mx(ap(out), ap(pl(out)), ap(a)), [a], [out, pl(out)], 12 + 0.22 * width(a))
+
+    def mm(bank, l, r, start=True, stop=True):
+        out = v("ps", 512 * bank, 512 * bank + width(r))
+        rec("t", lambda: g.tensor.matmul_mx(ap(out), ap(l), ap(pl(l)), ap(r), ap(pl(r)), start, stop), [l, pl(l), r, pl(r)], [out], 1.2 * (width(r) + 16))
+
+    def pick(out, win, off):
+        c = lambda x: x[:6] + (32,)
+        n = 1.3 * width(out)
+        rec("v", lambda: g.vector.tensor_copy(ap(c(out)), ap(c(win)).indirect(ap(off))), [win, off], [out], 50 + n)
+        rec("s", lambda: g.scalar.activation(ap(pl(out)), ap(pl(win)).indirect(ap(off)), AF.Copy), [pl(win), off], [pl(out)], 65 + n)
+
+    def dma(q, out, in_, reads, writes, after=()):
+        n = nd[0]
+        nd[0] += 1
+        rec(q, lambda: ENG[q].dma_start(out() if not isinstance(out, tuple) else ap(out), in_() if not isinstance(in_, tuple) else ap(in_)), reads, writes, 60, "d", "d%d" % n, 16, after)
+
+    def mxcopy(q, out, in_, after=()):
+        c = lambda x: x[:6] + (8,)
+        dma(q, c(out), c(in_), [in_], [out], after)
+        dma(q, pl(out), pl(in_), [pl(in_)], [pl(out)], after)
+
+    def send(peer, out, in_, key):
+        dst = T.cores[peer]
+        rid, pid, _ = topo.addr(dst)
+        m, n = topo.mask(core, dst), len(topo.engines(core, dst))
+        i = rec("g", lambda: g.remote_dma(ap(out), ap(in_), T.sem["a_" + key], T.sem["l_" + key], pid, rid, m), [in_], [], 120, "r", "l_" + key, n)
+        sent[key] = (i, out, len(topo.engines(dst, core)))
+
+    def sendmx(peer, out, in_, kc, ks):
+        c = lambda x: x[:6] + (8,)
+        send(peer, c(out), c(in_), kc)
+        send(peer, pl(out), pl(in_), ks)
+
+    def arrive(key):
+        i, out, n = sent[key]
+        rec(None, None, [], [out], 0, "a", "a_" + key, n, [i])
+
+    ps = lambda bank, a, b, s=1: v("ps", 512 * bank + a, 512 * bank + b, s)
+    pst = lambda bank, n, c: v("ps", 512 * bank + c, 512 * (bank + n - 1) + c + 1, 512)
+    col = lambda name, o=0: (lambda t: v(name, o + t, o + t + 1))
+    one = v("one", 0, 128)
+    eb = lambda b: v("eq", 128 * b, 128 * b + 128)
+
+    def iota(out, pattern, base, cm, flag=True):
+        kw = {"allow_small_or_imprecise_dtypes": True} if flag else {}
+        rec("g", lambda: g.iota(ap(out), pattern, base, cm, **kw), [], [out], 130 + 1.66 * width(out))
+
+    def select(out, in_, pattern, op, fillv, base, cm):
+        rec("g", lambda: g.affine_select(ap(out), ap(in_), pattern, op, fillv, base, cm), [in_], [out], 170 + 1.66 * width(out))
+
+    dma("y", v("ut"), lambda: T.u[:, 0:4], [], [v("ut")])
+    for c in range(4):
+        x = v("grt", 512 * c, 512 * c + 512)
+        dma("sy"[c % 2], x, (lambda c=c: T.gr[:, 512 * c:512 * c + 512]), [], [x])
+
+    fill(v("one"), 1.0)
+    fill(v("zt"))
+    fill(v("zo"), 0)
+    select(v("idt"), one, [[-1, 128]], OP.is_equal, 0.0, 0, 1)
+    fill(v("mone"), -0.5)
+    select(v("tri0"), v("mone"), [[1, 128]], OP.is_gt, 2.0, 0, -1)
+    iota(v("ni"), [[0, 1]], 0, 1, False)
+    iota(v("nf"), [[128, 4]], -256, 1)
+    iota(v("b511"), [[-128, 4]], 511, -1)
+    iota(v("i16"), [[0, 12], [1, 16]], 0, 0)
+    iota(v("i192"), [[1, K]], 0, 0)
+    iota(v("jf"), [[128, 3]], 0, 1)
+    iota(v("jw"), [[128, 3]], 16, 1, False)
+    iota(v("kw"), [[16, 12]], WA, 0)
+    ts(v("nl"), v("ni"), 15, OP.bitwise_and)
+    cp(v("nlf"), v("nl"))
+    nlf = v("nlf")
+    ts(v("nx"), v("nf"), nlf, OP.subtract)
+    for t in (1, 2, 3):
+        fill(v("c0t", t, 512 * t, 4))
+    fill(v("p0"))
+    quant(v("oneq"), v("one"))
+    ts(v("lk"), v("i16"), nlf, OP.is_equal, -1.0e6, OP.mult)
+    act(v("lk"), v("lk"), AF.Copy, bias=4096.0)
+    lift = lambda out, c, f=1.0: act(out, nlf, AF.Copy, scale=4096.0 * f, bias=c - 4096.0 * 15 * f)
+    lift(v("cn"), 256.0)
+    lift(v("cw"), float(MID))
+    lift(v("cz"), float(K))
+    lift(v("cth"), -0.5, -1.0)
+    ts(v("kw"), v("kw"), nlf, OP.add)
+    ts(v("jw"), v("jw"), 31, OP.bitwise_and)
+    cp(v("jwf"), v("jw"))
+    act(v("dl"), v("jwf"), AF.Copy, bias=-16.0)
+    tt(v("dh0"), v("jf"), v("jwf"), OP.subtract)
+    act(v("dh0"), v("dh0"), AF.Copy, bias=16.0 + WA - MID)
+    ts(v("isa"), v("jf"), K - 0.5, OP.is_gt)
+    act(v("nisa"), v("isa"), AF.Copy, scale=-1.0)
+    tt(v("basea"), v("jf"), v("isa"), OP.mult)
+    select(v("trit", 1, 1024, 4), v("one", 0, 256), [[1, 256]], OP.is_gt, 0.0, 0, -1)
+    select(v("trit", 2, 1024, 4), v("one", 0, 256), [[1, 256]], OP.is_gt, 0.0, -128, -1)
+    select(v("trit", 1, 1024, 4), v("trit", 1, 1024, 4), [[1, 256]], OP.not_equal, -960.0, 0, -1)
+    select(v("trit", 2, 1024, 4), v("trit", 2, 1024, 4), [[1, 256]], OP.not_equal, -960.0, -128, -1)
+    zero(v("trit", 0, 1024, 4))
+    zero(v("trit", 3, 1024, 4))
+    fill(v("ebf"))
+    act(v("ebf", 8, 520, 4), v("idt"), AF.Copy)
+    select(v("e2t"), v("ebf", 8, 520), [[1, 512]], OP.not_equal, 1.0, -2, -4)
+    for t in range(4):
+        act(v("nrept", 64 + t, 576, 4), one, AF.Identity, scale=v("nx", t, t + 1))
+    act(v("nrept", 576, 1088), v("one"), AF.Identity, scale=nlf)
+    fill(v("nrept", 0, 64))
+    for c in (1, 4):
+        act(v("nrept", 4 * c, 4 * c + 4), v("nx"), AF.Copy)
+        act(v("nrept", 4 * c + 8, 4 * c + 12), v("one", 0, 4), AF.Identity, scale=nlf)
+    act(v("nrept", 48, 49), v("isa", 1, 2), AF.Copy)
+    act(v("nrept", 49, 50), v("one", 0, 1), AF.Copy)
+    zero(v("dlt", 3, 512, 4))
+    for t in range(3):
+        act(v("dlt", t, 512, 4), one, AF.Identity, scale=v("dl", t, t + 1))
+    tt(v("jx", 0, 1), v("nx", 0, 1), v("isa", 1, 2), OP.mult)
+    tt(v("jx", 1, 2), nlf, v("isa", 1, 2), OP.mult)
+    for e, x in enumerate((v("jx", 0, 1), v("nx", 1, 2), v("jx", 1, 2), nlf)):
+        act(v("jdt", e, 512, 4), one, AF.Identity, scale=x)
+    for e in range(2):
+        select(v("idn", e, 4 * K, 4), v("one", 0, K), [[1, K]], OP.is_equal, 0.0, 64 - 128 * e, -1)
+        act(v("idn", 2 + e, 4 * K, 4), v("idn", e, 4 * K, 4), AF.Copy)
+    for k in range(2):
+        zero(v("misc", 416 * k, 416 * k + 416))
+    zero(v("urt", 0, 40))
+    for name, a, b, st in (("dht", 3, 512, 4), ("tau", 3, 4 * K, 4), ("st", 3, 4 * K, 4), ("ct", 3, 4 * K, 4), ("ordt", 3, 4 * 384, 4), ("rf0", 0, 1, 1), ("rf1", 0, 1, 1), ("na0", 2, 3, 1), ("na1", 2, 3, 1)):
+        zero(v(name, a, b, st))
+    act(v("dht", 2, 512, 4), one, AF.Identity, scale=v("dh0", 2, 3))
+    quant(v("zq"), v("zt", 0, 512))
+    for b in range(4):
+        quant(v("eq", 128 * b, 128 * b + 128), v("ebf", 8 - b, 520 - b))
+    quant(v("eq", 512, 640), v("e2t"))
+
+    for t in range(4):
+        ts(v("urt", 40 + t, 552, 4), one, v("ut", t, t + 1), OP.mult)
+    quant(v("ur"), v("urt", 40, 552))
+
+    def sizes(c):
+        qc = v("q0", 128 * c, 128 * c + 128)
+        i = quant(qc, v("grt", 512 * c, 512 * c + 512))
+        mm(4 + c % 3, qc, v("ur"))
+        mm(c, v("ur"), qc)
+        act(v("scol", c, c + 1), ps(4 + c % 3, 0, 1), AF.Abs)
+        act(v("srow", 128 * c, 128 * c + 128), ps(c, 0, 128), AF.Abs)
+        return i
+
+    def compare(c):
+        for t in [c] + list(range(c)):
+            blk = v("c0t", 512 * c + t, 512 * c + 512, 4)
+            row = v("srow", 128 * c, 128 * c + 128)
+            if t == c:
+                x = v("xd", 128 * c, 128 * c + 128)
+                act(x, row, AF.Sign, bias=v("scol", c, c + 1), scale=-1.0)
+                tt(blk, x, v("tri0"), OP.is_gt)
+            else:
+                ts(blk, row, v("scol", t, t + 1), OP.is_le)
+
+    def count(c):
+        for t in range(c + 1):
+            k = c * (c + 1) // 2 + t
+            act(v("junk", 128 * k, 128 * k + 128), v("c0t", 512 * c + t, 512 * c + 512, 4), AF.Copy, accum=v("p0", 4 * c + t, 4 * c + t + 1))
+        quant(v("c0q", 128 * c, 128 * c + 128), v("c0t", 512 * c, 512 * c + 512))
+        mm(c, v("c0q", 128 * c, 128 * c + 128), v("oneq"))
+        if c < 3:
+            tt(v("x%d" % c), v("b511") if c == 0 else v("x%d" % (c - 1)), v("p0", 4 * c, 4 * c + 4), OP.subtract)
+
+    early = [sizes(c) for c in range(4)]
+    for c in range(4):
+        compare(c)
+    for c in range(4):
+        count(c)
+    tt(v("x3"), pst(0, 4, 0), v("x2"), OP.add)
+    tt(v("rk0"), v("x3"), v("p0", 12, 16), OP.subtract)
+
+    def listof(bank, digits, onehot, scan, off, shift):
+        for k, d in enumerate(digits):
+            mm(bank, d, onehot, k == 0, k == len(digits) - 1)
+        row = ps(bank, 0, K)
+        rec("v", lambda: g.vector.tensor_tensor_scan(ap(scan), ap(v("lk")), ap(row), 0.0, OP.add, OP.max), [v("lk"), row], [scan], 0.83 * K)
+        last = (scan[0], scan[1] + 15, scan[2], 16) + scan[4:]
+        ts(off, last, shift, OP.add)
+        return last
+
+    for t in range(4):
+        ts(v("ot", t, 4 * K, 4), v("i192"), v("rk0", t, t + 1), OP.is_equal)
+    quant(v("oh", 64, 256), v("ot"))
+    for name, after in (("oh", early[0]), ("sq0", early[3])):
+        mxcopy("y", v(name, 0, 64), v("zq", 0, 64), [after])
+        mxcopy("y", v(name, 256, 320), v("zq", 0, 64), [after])
+    quant(v("nrep"), v("nrept", 64, 1088))
+    quant(v("ndcq"), v("nrept", 0, 576))
+    quant(v("idq"), v("idn"))
+    quant(v("jdq"), v("jdt"))
+
+    zone = {name: 48 * (6 - k) for k, name in enumerate(("nbt0", "ft0", "ndt0", "nbt1", "ft1", "ndt1", "xt"))}
+    mi = lambda name, a, b: v("misc", zone[name] + a, zone[name] + b)
+
+    def describe(s, peer, oh, digits):
+        hi, lo = v(digits, 4, 132), v(digits, 0, 128)
+        mm(4, v(oh, 0, 128), hi, True, False)
+        mm(4, v(oh, 128, 256), lo, False, True)
+        cp(mi("nbt" + s, 0, 8), ps(4, 0, 8))
+        i = quant(v("nbq" + s), mi("nbt" + s, 0, 512))
+        sendmx(peer, v("tl" + s, 0, 8), v("nbq" + s, 0, 8), "tc" + s, "ts" + s)
+        mm(5, v(oh, 64, 192), hi, True, False)
+        mm(5, v(oh, 192, 320), lo, False, True)
+        ts(v("nc" + s, 0, 1), ps(5, 0, 1), ps(5, 2, 3), OP.add)
+        ts(v("na" + s, 1, 2), ps(5, 1, 2), ps(5, 3, 4), OP.add)
+        if s == "1":
+            pick(v("rep"), v("nbq" + s), v("zo"))
+            mm(7, v("rep"), v("idq"))
+            act(v("nr" + s, 0, K), ps(7, 0, K), AF.Copy)
+        return i
+
+    def own(s):
+        for b in range(4):
+            mm(b, eb(b), v("win" + s, WA, WB), True, False)
+
+    def before(s, last):
+        w = "win" + s
+        arrive("tc" + s)
+        arrive("ts" + s)
+        mm(4, eb(4), v("tl" + s))
+        for e in range(4):
+            ts(v("mt" + s, e, 4 * K, 4), v("nr" + s, 0, K), ps(4, e % 2, e % 2 + 1), OP.is_equal)
+        quant(v("mtq" + s, 0, K), v("mt" + s))
+        scan = listof(7, (v("jdq"),), v("mtq" + s, 0, K), v("scb" + s), v("off1" + s), v("cz"))
+        act(v("bor" + s), ps(7, 0, K), AF.Sign, scale=-1.0)
+        ts(v("ub" + s), scan, v("cth"), OP.is_gt)
+        tt(v("ub2" + s), v("ub" + s), v("kw"), OP.mult)
+        cp(v("offb" + s), v("ub2" + s))
+        pick(v("an" + s), v(w, 0, WB), v("offb" + s))
+        tt(v("nc" + s, 1, 3), v("na" + s, 1, 3), ps(4, 0, 2), OP.add)
+        mm(5, v("mtq" + s, 0, 128), v("ndcq", 12, 140), True, False)
+        mm(5, v("mtq" + s, 128, 256), v("ndcq", 10, 138), False, True)
+        both = ps(5, 0, 3, 2)
+        ts(v("keep" + s), both, -1.0, OP.mult, 1.0, OP.add)
+        ts(v("fm" + s), both, float(WM - WA), OP.mult)
+        tt(v("dhr" + s), v("fm" + s), v("dh0", 0, 2), OP.add)
+        for t in range(2):
+            act(v("dht", t, 512, 4), one, AF.Identity, scale=v("dhr" + s, t, t + 1))
+            k = 2 * int(s) + t
+            act(v("junk3", K * k, K * k + K), v("mt" + s, t, 4 * K, 4), AF.Copy, accum=v("du" + s, t, t + 1))
+        quant(v("dhq" + s), v("dht"))
+        tt(mi("ft" + s, 9, 11), v("du" + s), v("isa", 1, 3), OP.mult)
+        ts(v("fo" + s), mi("ft" + s, 8, 11), 2.0, OP.mult, -0.5, OP.add)
+        quant(v("ftq" + s), mi("ft" + s, 0, 544))
+        mm(6, v("triq", 0, 128), v("ftq" + s, 2, 130), True, False)
+        mm(6, v("triq", 128, 256), v("ftq" + s, 0, 128), False, True)
+        tt(v("bs" + s, 1, 3), v("basea", 1, 3), ps(6, 0, 3, 2), OP.subtract)
+        for t in range(3):
+            ts(v("tau", t, 4 * K, 4), v("nr" + s, 0, K), v("nc" + s, t, t + 1), OP.is_le, v("fo" + s, t, t + 1), OP.add)
+        quant(v("tauq" + s), v("tau"))
+        n = mi("ndt" + s, 4, 7)
+        ts(n, v("nc" + s), ROUND16, OP.add, -ROUND16, OP.add)
+        tt(mi("ndt" + s, 12, 15), v("nc" + s), n, OP.subtract)
+        act(mi("ndt" + s, 16, 19), n, AF.Copy)
+        act(mi("ndt" + s, 24, 27), mi("ndt" + s, 12, 15), AF.Copy)
+        quant(v("ndq" + s), mi("ndt" + s, 0, 544))
+        if last:
+            pick(v("repb"), v("tl" + s), v("zo"))
+            mm(6, v("repb"), v("idq"))
+            act(v("nr" + s, K, 2 * K), ps(6, 0, K), AF.Copy)
+            ts(v("nnc"), v("nc" + s), -1.0, OP.mult)
+            for t in range(3):
+                act(v("ordt", t, 4 * 384, 4), v("nr" + s), AF.Sign, bias=v("nnc", t, t + 1))
+            quant(v("ordq"), v("ordt"))
+        for t in range(3):
+            mm(4 + t, eb(t), v("tauq" + s))
+
+    def merge(s):
+        w, bp, an = "win" + s, "bp" + s, "an" + s
+        arrive("wc" + s)
+        arrive("ws" + s)
+        for t in range(3):
+            mm(7, v(w, WA + 128 * t, WA + 128 * t + 128), v("uq", 4 - 2 * t, 132 - 2 * t), t == 0, t == 2)
+        tt(v("bi" + s), ps(7, 0, 3, 2), v("keep" + s), OP.mult)
+        act(v("acol" + s, 2, 3), ps(7, 4, 5), AF.Abs)
+        pick(v(bp), v(w, WB, WM), v("off1" + s))
+        for b in range(4):
+            mm(b, eb(b), v(bp), False, True)
+            tt(v("ht" + s, b, 4 * K, 4), ps(b, 0, K), v("bor" + s), OP.mult)
+        quant(v(w, WM, WM + K), v("ht" + s))
+        ur = v("ur")
+        mm(7, ur, v(an), True, False)
+        mm(7, ur, v(w, WM, WM + K), False, True)
+        for t in range(2):
+            mm(0, v(w, WM + 128 * t, WM + 128 * t + 128), v("uq", 4 - 2 * t, 132 - 2 * t), t == 0, t == 1)
+        act(v("arow" + s), ps(7, 0, K), AF.Abs)
+        for t in range(2):
+            act(v("acol" + s, t, t + 1), ps(0, 2 * t, 2 * t + 1), AF.Abs, bias=v("bi" + s, t, t + 1))
+        for t in (2, 0, 1):
+            x = v("v" + s, K * t, K * t + K)
+            act(x, v("arow" + s), AF.Sign, bias=v("acol" + s, t, t + 1), scale=-1.0)
+            tt(v("ct", t, 4 * K, 4), x, ps(4 + t, 0, K), OP.is_gt)
+        for t in (2, 1):
+            k = 2 * int(s) + t - 1
+            act(v("junk2", K * k, K * k + K), v("ct", t, 4 * K, 4), AF.Identity, scale=v("nisa", t, t + 1), accum=v("rs" + s, t, t + 1))
+        quant(v("cq" + s, 0, K), v("ct"))
+        mm(1, v("cq" + s, 0, 128), v("oneq"))
+        mm(2, v("cq" + s, 128, 256), v("oneq"))
+        tt(v("rf" + s, 1, 3), v("bs" + s, 1, 3), v("rs" + s, 1, 3), OP.add)
+        tt(v("rf" + s, 0, 2), pst(1, 2, 0), v("rf" + s, 0, 2), OP.add)
+
+    def place(s, places):
+        for t in range(3):
+            ts(v("st", t, 4 * K, 4), v("i192"), places(t), OP.is_equal)
+        quant(v("sq" + s, 64, 256), v("st"))
+
+    def chosen(s, out):
+        listof(6, (v("dhq" + s), v("dlq")), v("sq" + s, 64, 256), v("scs" + s), v("offs" + s), v("cw"))
+        pick(out, v("win" + s), v("offs" + s))
+
+    mark = describe("0", rank ^ 1, "oh", "ndcq")
+    listof(6, (v("nrep", 0, 128), v("nrep", 128, 256)), v("oh", 64, 256), v("sc"), v("off0"), v("cn"))
+    act(v("nr0", 0, K), ps(6, 0, K), AF.Copy)
+    pick(v("win0", WA, WB), v("q0"), v("off0"))
+    sendmx(rank ^ 1, v("win0", WB, WZ), v("win0", WA, WB), "wc0", "ws0")
+    for s in "01":
+        after = early[3] if s == "0" else mark
+        mxcopy("y", v("tl" + s, 8, 128), v("zq", 0, 120), [after])
+        mxcopy("y", v("mtq" + s, K, 256), v("zq", 0, 256 - K), [after])
+        mxcopy("y", v("cq" + s, K, 256), v("zq", 0, 256 - K), [after])
+        mxcopy("y", v("win" + s, 0, WA), v("zq", 0, WA), [after])
+        mxcopy("y", v("win" + s, WZ, WM), v("zq", 0, WM - WZ), [after])
+        mxcopy("y", v("win" + s, WY, WE), v("zq", 0, WE - WY), [after])
+    dma("y", v("wt"), lambda: T.w[:, :], [], [v("wt")], [mark])
+    act(v("urt", 16, 20), v("ut"), AF.Copy)
+    quant(v("uq"), v("urt", 0, 544))
+    quant(v("triq"), v("trit"))
+    quant(v("dlq"), v("dlt"))
+    own("0")
+    before("0", False)
+    merge("0")
+
+    place("0", col("rf0"))
+    describe("1", rank ^ 2, "sq0", "ndq0")
+    chosen("0", v("win1", WA, WB))
+    sendmx(rank ^ 2, v("win1", WB, WZ), v("win1", WA, WB), "wc1", "ws1")
+    quant(v("wq"), v("wt"))
+    own("1")
+    before("1", True)
+    merge("1")
+
+    ts(mi("xt", 0, 3), v("rf1"), K - 0.5, OP.is_lt, 0.5, OP.mult)
+    quant(v("xq"), mi("xt", 0, 512))
+    ts(v("ntk"), v("rf1"), K - 0.5, OP.is_gt, 1024.0, OP.mult)
+    for c in range(3):
+        mm(c, v("ordq", 128 * c, 128 * c + 128), v("xq"))
+    ts(v("ntk2"), v("ntk"), (K - 1) / 2, OP.add)
+    tt(v("plc"), pst(0, 3, 0), v("ntk2"), OP.add)
+    fin = v("fin")
+    place("1", col("plc"))
+    chosen("1", fin)
+    mm(4, v("ndq1", 4, 132), v("sq1", 64, 256), True, False)
+    mm(4, v("ndq1", 6, 134), v("sq1", 64, 256), False, True)
+    ts(v("nbw", 0, K, 1, 0, 1), v("ps", 4 * 512, 4 * 512 + K, 1, 0, 1), 256.0, OP.add)
+    dma("y", lambda: T.nb[:, :], lambda: T.nbw[0:1, :], [v("nbw", 0, K, 1, 0, 1)], [])
+    dma("y", lambda: T.oc[:, :], lambda: T.fin[:, :].bitcast(dt.uint8), [fin], [])
+    for k in range(4):
+        dma("sy"[k % 2], (lambda k=k: T.osc[4 * k:4 * k + 4, :]), (lambda k=k: T.fins[32 * k:32 * k + 4, :]), [pl(fin)], [])
+    for o in range(O):
+        mm(5 + 2 * o, v("wq", 128 * o, 128 * o + 128), fin)
+    act(v("yb", 0, K), ps(5, 0, K), AF.Copy)
+    cp(v("yb", K, 2 * K), ps(7, 0, K))
+    dma("s", lambda: T.y[:, 0:K], v("yb", 0, K), [v("yb", 0, K)], [])
+    dma("y", lambda: T.y[:, K:2 * K], v("yb", K, 2 * K), [v("yb", K, 2 * K)], [])
+
+    acc, edges = {}, []
+    for i, r in enumerate(prog):
+        e = {j: True for j in r["after"] if r["kind"] != "a"}
+        for regs, w in ((r["reads"], False), (r["writes"], True)):
+            for x in regs:
+                for (y, yw, j) in acc.get(x[0], ()):
+                    if j == i or not (w or yw or x[0] == "ps") or not overlap(x, y):
+                        continue
+                    if prog[j]["q"] == r["q"] and prog[j]["kind"] == "c" and r["kind"] == "c":
+                        wait = yw and not (r["q"] == "t" and x[0] == "ps")
+                    else:
+                        wait = w or yw or x[0] == "ps"
+                    if x[0] == "ps" and not w and not yw and prog[j]["q"] == r["q"]:
+                        continue
+                    e[j] = e.get(j, False) or wait
+        edges.append(e)
+        for x in r["reads"]:
+            acc.setdefault(x[0], []).append((x, False, i))
+        for x in r["writes"]:
+            acc.setdefault(x[0], []).append((x, True, i))
+
+    n = len(prog)
+    preds = [dict(e) for e in edges]
+    for i, r in enumerate(prog):
+        if r["kind"] == "a":
+            preds[i][r["after"][0]] = True
+    succ = [[] for _ in prog]
+    for i, e in enumerate(preds):
+        for j, wait in e.items():
+            succ[j].append((i, wait))
+
+    def guess(compute, product, wake, same, local, link):
+        cost = [r["cost"] * (product if r["q"] == "t" else 1.0 if r["kind"] != "c" else compute) for r in prog]
+        lag = {"c": 0.0, "d": local, "r": link, "a": 0.0}
+        gaps = [{j: (0.0 if not wait else lag[prog[j]["kind"]] + (same if prog[j]["q"] == prog[i]["q"] and prog[j]["kind"] == "c" else wake)) for j, wait in e.items()} for i, e in enumerate(preds)]
+        return cost, lag, gaps, cost, [lag[r["kind"]] for r in prog], [[(j, d) for j, d in e.items() if d] for e in gaps]
+
+    qn = {q: k for k, q in enumerate("vstgy")}
+    queue = [qn.get(r["q"], 5) for r in prog]
+
+    def length(order, model):
+        cost, lag, gaps = model[3:]
+        end, free, top = [0.0] * n, [0.0] * 6, 0.0
+        for i in order:
+            q = queue[i]
+            x = free[q] if q < 5 else 0.0
+            for j, d in gaps[i]:
+                y = end[j] + d
+                if y > x:
+                    x = y
+            x += cost[i]
+            end[i] = free[q] = x
+            if x + lag[i] > top:
+                top = x + lag[i]
+        return top
+
+    def total(order):
+        return sum([length(order, m) / b for m, b in zip(models, BASE)])
+
+    def arrange(model, weight, margin, soon):
+        cost, lag, gaps = model[:3]
+        tail = [0.0] * n
+        for j in range(n - 1, -1, -1):
+            tail[j] = max([tail[i] + gaps[i][j] for i, wait in succ[j]] + [lag[prog[j]["kind"]]]) + cost[j]
+        urge = [t * w for t, w in zip(tail, weight)]
+        left, ready, end, free, order = [len(e) for e in preds], {}, [0.0] * n, {}, []
+        for i in range(n):
+            if not left[i]:
+                ready.setdefault(prog[i]["q"], {})[i] = 0.0
+        for _ in range(n):
+            best = None
+            for q, calls in ready.items():
+                if not calls:
+                    continue
+                f = free.get(q, 0.0) if q else 0.0
+                top = max(urge[i] for i in calls)
+                c = [(max(f, t + (margin if urge[i] < top - 1500.0 else 0.0)), -urge[i], i) for i, t in calls.items()]
+                first = min(c)[0]
+                for x in sorted((x for x in c if x[0] <= first + soon), key=lambda x: x[1]):
+                    e = x[0] + cost[x[2]]
+                    if not any(y[0] < e - soon and y[1] < x[1] - 300.0 for y in c):
+                        break
+                else:
+                    x = min((y for y in c if y[0] <= first + soon), key=lambda y: y[1])
+                if best is None or x < best:
+                    best = x
+            i = best[2]
+            q = prog[i]["q"]
+            t = ready[q].pop(i)
+            end[i] = max(t, free.get(q, 0.0) if q else 0.0) + cost[i]
+            free[q] = end[i]
+            order.append(i)
+            for k, wait in succ[i]:
+                left[k] -= 1
+                if not left[k]:
+                    ready.setdefault(prog[k]["q"], {})[k] = max(end[j] + d if d else end[j] - cost[j] for j, d in gaps[k].items())
+        return order
+
+    if "order" not in ORDER:
+        models = [guess(*x) for x in GUESSES]
+        state, found = 1, None
+        for trial in range(TRIALS):
+            weight = []
+            for i in range(n):
+                state = (state * 1103515245 + 12345) % 2 ** 31
+                weight.append(1.0 + (state / 2.0 ** 31 - 0.5) * (0.0, 0.02, 0.05, 0.1)[trial % 4])
+            o = arrange(models[trial % len(models)], weight, (0.0, 80.0, 160.0, 240.0, 320.0)[trial % 5], (30.0, 60.0, 100.0)[trial % 3])
+            t = total(o)
+            if found is None or t < found[0]:
+                found = (t, o)
+        t, order = found
+        state, place = 7, {i: k for k, i in enumerate(order)}
+        for trial in range(MOVES):
+            state = (state * 1103515245 + 12345) % 2 ** 31
+            a = (state >> 8) % n
+            i = order[a]
+            lo = max([place[j] + 1 for j in preds[i]] + [a - 60, 0])
+            hi = min([place[k] - 1 for k, _ in succ[i]] + [a + 60, n - 1])
+            state = (state * 1103515245 + 12345) % 2 ** 31
+            b = lo + (state >> 8) % (hi - lo + 1)
+            if a == b:
+                continue
+            o = list(order)
+            o.pop(a)
+            o.insert(b, i)
+            t2 = total(o)
+            if t2 <= t:
+                t, order = t2, o
+                for k in range(min(a, b), max(a, b) + 1):
+                    place[o[k]] = k
+        ORDER["order"] = order
+        ORDER["found"] = t
+    order = ORDER["order"]
+    place = {i: k for k, i in enumerate(order)}
+    deps = [sorted(place[j] for j, wait in edges[i].items() if wait) for i in order]
+    prog = [prog[i] for i in order]
+
+    know, snap, need, used = {}, [], [], set()
+    key = lambda i: (prog[i]["q"], i) if prog[i]["kind"] == "c" else (i, 0)
+    for i, r in enumerate(prog):
+        k = know.setdefault(r["q"], {}) if r["q"] else {}
+        last = {}
+        for d in deps[i]:
+            a, m = key(d)
+            if k.get(a, -1) < m and (a not in last or key(last[a])[1] < m):
+                last[a] = d
+        ds = sorted(last.values())
+        ds = [d for d in ds if not any(e != d and snap[e].get(key(d)[0], -1) >= key(d)[1] for e in ds)]
+        for d in ds:
+            used.add(d)
+            for a, m in snap[d].items():
+                if k.get(a, -1) < m:
+                    k[a] = m
+        s = dict(k)
+        s[key(i)[0]] = key(i)[1]
+        snap.append(s)
+        need.append(ds)
+    lastc = {r["q"]: i for i, r in enumerate(prog) if r["kind"] == "c"}
+    used |= set(lastc.values())
+    total, val = {q: 0 for q in lastc}, {}
+    for i, r in enumerate(prog):
+        if r["q"] is None:
+            continue
+        e = ENG[r["q"]]
+        for d in need[i]:
+            p = prog[d]
+            if p["kind"] == "c":
+                e.wait_ge(T.sem["q_" + p["q"]], val[d])
+            else:
+                e.wait_ge(T.sem[p["sem"]], p["amount"])
+        ins = r["fn"]()
+        if r["kind"] == "c" and i in used:
+            total[r["q"]] += 1
+            val[i] = total[r["q"]]
+            ins.then_inc(T.sem["q_" + r["q"]], 1)
+        elif r["kind"] == "d":
+            ins.then_inc(T.sem[r["sem"]], 16)
+    for q in total:
+        g.wait_ge(T.sem["q_" + q], total[q])
+    for r in prog:
+        if r["kind"] in "dra":
+            g.wait_ge(T.sem[r["sem"]], r["amount"])

@@ -10,12 +10,12 @@ SCRATCH = {"ps": ("psum", [128, 4096], F32)}
 PLACE = {}
 _TOP = {}
 _ALIGN = {BF: 16, F32: 8, I32: 8, U16: 16}
-_ALONE = ("ut", "urt", "grt", "wt", "nbw", "yb")
+_ALONE = ("ut", "urt", "grt", "wt", "nbw", "yb", "yw0", "yw1")
 _CONST = []
 ORDER = {}
 TRIALS, MOVES = 60, 24000
-GUESSES = ((1.0, 1.0, 100.0, 0.0, 1500.0, 1700.0), (1.2, 1.2, 60.0, 20.0, 2000.0, 2500.0), (1.0, 0.8, 200.0, 50.0, 1500.0, 2000.0), (1.3, 1.6, 100.0, 50.0, 1500.0, 2000.0))
-BASE = (29700.0, 35200.0, 34000.0, 40900.0)
+GUESSES = ((1.0, 1.0, 200.0, 100.0, 1500.0, 1500.0, 1200.0), (1.2, 1.2, 100.0, 50.0, 2000.0, 2000.0, 1500.0), (1.0, 0.7, 300.0, 150.0, 1300.0, 1500.0, 1000.0), (1.3, 1.4, 150.0, 50.0, 1500.0, 2000.0, 2000.0))
+BASE = (35000.0, 36000.0, 37000.0, 41000.0)
 
 
 def _buf(name, n, t):
@@ -37,7 +37,7 @@ def _mx(name, n):
 
 
 for _n, _w, _t in (
-        ("one", 512, BF), ("zt", 544, BF), ("i16", K, BF), ("i192", K, BF), ("idt", 128, BF), ("ebf", 528, BF), ("e2t", 512, BF), ("mone", 128, BF), ("tri0", 128, BF),
+        ("one", 512, BF), ("zt", 544, BF), ("i16", K, BF), ("i192", K, BF), ("i2", K, BF), ("idt", 128, BF), ("ebf", 528, BF), ("e2t", 512, BF), ("mone", 128, BF), ("tri0", 128, BF),
         ("ni", 1, I32), ("nl", 1, I32), ("nf", 4, F32), ("nlf", 1, F32), ("nx", 4, F32), ("nrept", 1088, BF), ("dlt", 512, BF), ("trit", 1024, BF),
         ("jx", 2, F32), ("jdt", 512, BF), ("idn", 4 * K, BF), ("zo", 8, U16),
         ("kw", 12, F32), ("jw", 3, I32), ("jf", 3, F32), ("jwf", 3, F32), ("dl", 3, F32), ("dh0", 3, F32),
@@ -48,9 +48,9 @@ for _n, _w, _t in (
 for _n, _w, _t in (
         ("ut", 4, BF), ("urt", 552, BF), ("grt", 4 * P, BF), ("wt", 1024, BF),
         ("srow", P, F32), ("scol", 4, F32), ("xd", 512, BF), ("c0t", 4 * P, BF), ("p0", 16, F32), ("junk", 10 * 128, BF), ("junk2", 4 * K, BF), ("junk3", 4 * K, BF),
-        ("x0", 4, F32), ("x1", 4, F32), ("x2", 4, F32), ("x3", 4, F32), ("rk0", 4, F32), ("ot", 4 * K, BF), ("sc", K, F32), ("off0", 12, U16),
+        ("x1", 4, F32), ("x2", 4, F32), ("x3", 4, F32), ("ot", 4 * K, BF), ("sc", K, F32), ("off0", 12, U16),
         ("ordt", 4 * 384, BF), ("nnc", 3, F32), ("misc", 832, BF), ("dht", 512, BF), ("tau", 4 * K, BF), ("ct", 4 * K, BF), ("st", 4 * K, BF),
-        ("ntk", 3, F32), ("ntk2", 3, F32), ("plc", 3, F32), ("nbw", K, F32), ("yb", O * K, F32)):
+        ("ntk", 3, F32), ("plc", 3, F32), ("nbw", K, F32), ("yb", O * K, F32), ("yw0", WY, F32), ("yw1", WY, F32)):
     _buf(_n, _w, _t)
 for _n, _w in (("ur", 128), ("uq", 136), ("q0", P), ("wq", 256), ("oneq", 128), ("zq", 128), ("nrep", 256), ("dlq", 128), ("eq", 640), ("triq", 256),
                ("jdq", 128), ("idq", K), ("ndcq", 144), ("c0q", P), ("oh", 320), ("ordq", 384), ("xq", 128), ("rep", 128), ("repb", 128), ("fin", K)):
@@ -154,11 +154,16 @@ def rank_program(g, core, T, topo):
         out = v("ps", 512 * bank, 512 * bank + width(r))
         rec("t", lambda: g.tensor.matmul_mx(ap(out), ap(l), ap(pl(l)), ap(r), ap(pl(r)), start, stop), [l, pl(l), r, pl(r)], [out], 1.2 * (width(r) + 16))
 
-    def pick(out, win, off):
-        c = lambda x: x[:6] + (32,)
+    def gather(q, out, win, off, c=lambda x: x):
         n = 1.3 * width(out)
-        rec("v", lambda: g.vector.tensor_copy(ap(c(out)), ap(c(win)).indirect(ap(off))), [win, off], [out], 50 + n)
-        rec("s", lambda: g.scalar.activation(ap(pl(out)), ap(pl(win)).indirect(ap(off)), AF.Copy), [pl(win), off], [pl(out)], 65 + n)
+        if q == "v":
+            rec("v", lambda: g.vector.tensor_copy(ap(c(out)), ap(c(win)).indirect(ap(off))), [win, off], [out], 50 + n)
+        else:
+            rec("s", lambda: g.scalar.activation(ap(out), ap(win).indirect(ap(off)), AF.Copy), [win, off], [out], 65 + n)
+
+    def pick(out, win, off):
+        gather("v", out, win, off, lambda x: x[:6] + (32,))
+        gather("s", pl(out), pl(win), off)
 
     def dma(q, out, in_, reads, writes, after=()):
         n = nd[0]
@@ -188,7 +193,6 @@ def rank_program(g, core, T, topo):
 
     ps = lambda bank, a, b, s=1: v("ps", 512 * bank + a, 512 * bank + b, s)
     pst = lambda bank, n, c: v("ps", 512 * bank + c, 512 * (bank + n - 1) + c + 1, 512)
-    col = lambda name, o=0: (lambda t: v(name, o + t, o + t + 1))
     one = v("one", 0, 128)
     eb = lambda b: v("eq", 128 * b, 128 * b + 128)
 
@@ -273,16 +277,21 @@ def rank_program(g, core, T, topo):
     for k in range(2):
         zero(v("misc", 416 * k, 416 * k + 416))
     zero(v("urt", 0, 40))
-    for name, a, b, st in (("dht", 3, 512, 4), ("tau", 3, 4 * K, 4), ("st", 3, 4 * K, 4), ("ct", 3, 4 * K, 4), ("ordt", 3, 4 * 384, 4), ("rf0", 0, 1, 1), ("rf1", 0, 1, 1), ("na0", 2, 3, 1), ("na1", 2, 3, 1)):
+    for name, a, b, st in (("dht", 3, 512, 4), ("tau", 3, 4 * K, 4), ("st", 3, 4 * K, 4), ("ct", 3, 4 * K, 4), ("ordt", 3, 4 * 384, 4), ("rf1", 0, 1, 1), ("na0", 2, 3, 1), ("na1", 2, 3, 1),
+                           ("yw0", 0, WA, 1), ("yw0", WZ, WM, 1), ("yw1", 0, WA, 1), ("yw1", WZ, WM, 1)):
         zero(v(name, a, b, st))
     act(v("dht", 2, 512, 4), one, AF.Identity, scale=v("dh0", 2, 3))
+    act(v("i2"), v("i192"), AF.Copy, scale=2.0, bias=1.0 - K)
     quant(v("zq"), v("zt", 0, 512))
     for b in range(4):
         quant(v("eq", 128 * b, 128 * b + 128), v("ebf", 8 - b, 520 - b))
     quant(v("eq", 512, 640), v("e2t"))
 
     for t in range(4):
-        ts(v("urt", 40 + t, 552, 4), one, v("ut", t, t + 1), OP.mult)
+        if t < 2:
+            ts(v("urt", 40 + t, 552, 4), one, v("ut", t, t + 1), OP.mult)
+        else:
+            act(v("urt", 40 + t, 552, 4), v("zt", 0, 128), AF.Identity, bias=v("ut", t, t + 1))
     quant(v("ur"), v("urt", 40, 552))
 
     def sizes(c):
@@ -298,29 +307,31 @@ def rank_program(g, core, T, topo):
         for t in [c] + list(range(c)):
             blk = v("c0t", 512 * c + t, 512 * c + 512, 4)
             row = v("srow", 128 * c, 128 * c + 128)
-            if t == c:
-                x = v("xd", 128 * c, 128 * c + 128)
+            x = v("xd", 128 * c, 128 * c + 128)
+            if t == c == 3:
                 act(x, row, AF.Sign, bias=v("scol", c, c + 1), scale=-1.0)
                 tt(blk, x, v("tri0"), OP.is_gt)
+            elif t == c:
+                ts(x, row, v("scol", t, t + 1), OP.is_le)
+                select(blk, x, [[1, 128]], OP.is_gt, 0.0, 0, -1)
             else:
                 ts(blk, row, v("scol", t, t + 1), OP.is_le)
 
     def count(c):
-        for t in range(c + 1):
+        for t in range(c + 1) if c else ():
             k = c * (c + 1) // 2 + t
-            act(v("junk", 128 * k, 128 * k + 128), v("c0t", 512 * c + t, 512 * c + 512, 4), AF.Copy, accum=v("p0", 4 * c + t, 4 * c + t + 1))
+            d = 128 if k == 1 else 0
+            act(v("junk", 128 * k - d, 128 * k + 128), v("c0t", 512 * c + t - 4 * d, 512 * c + 512, 4), AF.Copy, accum=v("p0", 4 * c + t, 4 * c + t + 1))
         quant(v("c0q", 128 * c, 128 * c + 128), v("c0t", 512 * c, 512 * c + 512))
         mm(c, v("c0q", 128 * c, 128 * c + 128), v("oneq"))
-        if c < 3:
-            tt(v("x%d" % c), v("b511") if c == 0 else v("x%d" % (c - 1)), v("p0", 4 * c, 4 * c + 4), OP.subtract)
+        if c:
+            tt(v("x%d" % c), v("b511") if c == 1 else v("x%d" % (c - 1)), v("p0", 4 * c, 4 * c + 4), OP.subtract)
 
     early = [sizes(c) for c in range(4)]
     for c in range(4):
         compare(c)
     for c in range(4):
         count(c)
-    tt(v("x3"), pst(0, 4, 0), v("x2"), OP.add)
-    tt(v("rk0"), v("x3"), v("p0", 12, 16), OP.subtract)
 
     def listof(bank, digits, onehot, scan, off, shift):
         for k, d in enumerate(digits):
@@ -332,7 +343,7 @@ def rank_program(g, core, T, topo):
         return last
 
     for t in range(4):
-        ts(v("ot", t, 4 * K, 4), v("i192"), v("rk0", t, t + 1), OP.is_equal)
+        ts(v("ot", t, 4 * K, 4), v("i192"), ps(t, 0, 1), OP.subtract, v("x3", t, t + 1), OP.is_equal)
     quant(v("oh", 64, 256), v("ot"))
     for name, after in (("oh", early[0]), ("sq0", early[3])):
         mxcopy("y", v(name, 0, 64), v("zq", 0, 64), [after])
@@ -415,7 +426,7 @@ def rank_program(g, core, T, topo):
             for t in range(3):
                 act(v("ordt", t, 4 * 384, 4), v("nr" + s), AF.Sign, bias=v("nnc", t, t + 1))
             quant(v("ordq"), v("ordt"))
-        for t in range(3):
+        for t in (1, 2):
             mm(4 + t, eb(t), v("tauq" + s))
 
     def merge(s):
@@ -423,9 +434,10 @@ def rank_program(g, core, T, topo):
         arrive("wc" + s)
         arrive("ws" + s)
         for t in range(3):
-            mm(7, v(w, WA + 128 * t, WA + 128 * t + 128), v("uq", 4 - 2 * t, 132 - 2 * t), t == 0, t == 2)
-        tt(v("bi" + s), ps(7, 0, 3, 2), v("keep" + s), OP.mult)
-        act(v("acol" + s, 2, 3), ps(7, 4, 5), AF.Abs)
+            mm(4, v(w, WA + 128 * t, WA + 128 * t + 128), v("uq", 4 - 2 * t, 132 - 2 * t), t == 0, t == 2)
+        tt(v("bi" + s), ps(4, 0, 3, 2), v("keep" + s), OP.mult)
+        act(v("acol" + s, 2, 3), ps(4, 4, 5), AF.Abs)
+        mm(4, eb(0), v("tauq" + s))
         pick(v(bp), v(w, WB, WM), v("off1" + s))
         for b in range(4):
             mm(b, eb(b), v(bp), False, True)
@@ -447,19 +459,23 @@ def rank_program(g, core, T, topo):
             k = 2 * int(s) + t - 1
             act(v("junk2", K * k, K * k + K), v("ct", t, 4 * K, 4), AF.Identity, scale=v("nisa", t, t + 1), accum=v("rs" + s, t, t + 1))
         quant(v("cq" + s, 0, K), v("ct"))
-        mm(1, v("cq" + s, 0, 128), v("oneq"))
         mm(2, v("cq" + s, 128, 256), v("oneq"))
+        mm(1, v("cq" + s, 0, 128), v("oneq"))
         tt(v("rf" + s, 1, 3), v("bs" + s, 1, 3), v("rs" + s, 1, 3), OP.add)
-        tt(v("rf" + s, 0, 2), pst(1, 2, 0), v("rf" + s, 0, 2), OP.add)
 
-    def place(s, places):
+    def place(s, row, places):
         for t in range(3):
-            ts(v("st", t, 4 * K, 4), v("i192"), places(t), OP.is_equal)
+            ts(v("st", t, 4 * K, 4), v(row), *places[t])
         quant(v("sq" + s, 64, 256), v("st"))
 
     def chosen(s, out):
         listof(6, (v("dhq" + s), v("dlq")), v("sq" + s, 64, 256), v("scs" + s), v("offs" + s), v("cw"))
         pick(out, v("win" + s), v("offs" + s))
+
+    def weigh(a, banks):
+        for o in range(O):
+            mm(banks[o], v("wq", 128 * o, 128 * o + 128), v("win1", a, a + K))
+            act(v("yw%d" % o, a, a + K), ps(banks[o], 0, K), AF.Copy)
 
     mark = describe("0", rank ^ 1, "oh", "ndcq")
     listof(6, (v("nrep", 0, 128), v("nrep", 128, 256)), v("oh", 64, 256), v("sc"), v("off0"), v("cn"))
@@ -483,25 +499,30 @@ def rank_program(g, core, T, topo):
     before("0", False)
     merge("0")
 
-    place("0", col("rf0"))
+    place("0", "i192", ((ps(1, 0, 1), OP.is_equal), (ps(2, 0, 1), OP.subtract, v("rf0", 1, 2), OP.is_equal), (v("rf0", 2, 3), OP.is_equal)))
     describe("1", rank ^ 2, "sq0", "ndq0")
     chosen("0", v("win1", WA, WB))
     sendmx(rank ^ 2, v("win1", WB, WZ), v("win1", WA, WB), "wc1", "ws1")
     quant(v("wq"), v("wt"))
     own("1")
+    weigh(WA, (5, 6))
     before("1", True)
     merge("1")
+    weigh(WB, (3, 7))
+    weigh(WM, (3, 7))
 
-    ts(mi("xt", 0, 3), v("rf1"), K - 0.5, OP.is_lt, 0.5, OP.mult)
+    ts(v("plc"), v("rf1"), -1.0, OP.mult, K - 0.5, OP.add)
+    ts(mi("xt", 2, 3), v("plc", 2, 3), 0.0, OP.is_gt)
+    tt(mi("xt", 0, 2), pst(1, 2, 0), v("plc", 0, 2), OP.is_lt)
     quant(v("xq"), mi("xt", 0, 512))
-    ts(v("ntk"), v("rf1"), K - 0.5, OP.is_gt, 1024.0, OP.mult)
+    ts(v("ntk"), mi("xt", 0, 3), -1024.0, OP.mult, 1024.0, OP.add)
     for c in range(3):
         mm(c, v("ordq", 128 * c, 128 * c + 128), v("xq"))
-    ts(v("ntk2"), v("ntk"), (K - 1) / 2, OP.add)
-    tt(v("plc"), pst(0, 3, 0), v("ntk2"), OP.add)
     fin = v("fin")
-    place("1", col("plc"))
+    place("1", "i2", [(ps(t, 0, 1), OP.subtract, v("ntk", t, t + 1), OP.is_equal) for t in range(3)])
     chosen("1", fin)
+    for o in range(O):
+        gather("vs"[o], v("yb", K * o, K * o + K), v("yw%d" % o), v("offs1"))
     mm(4, v("ndq1", 4, 132), v("sq1", 64, 256), True, False)
     mm(4, v("ndq1", 6, 134), v("sq1", 64, 256), False, True)
     ts(v("nbw", 0, K, 1, 0, 1), v("ps", 4 * 512, 4 * 512 + K, 1, 0, 1), 256.0, OP.add)
@@ -509,12 +530,8 @@ def rank_program(g, core, T, topo):
     dma("y", lambda: T.oc[:, :], lambda: T.fin[:, :].bitcast(dt.uint8), [fin], [])
     for k in range(4):
         dma("sy"[k % 2], (lambda k=k: T.osc[4 * k:4 * k + 4, :]), (lambda k=k: T.fins[32 * k:32 * k + 4, :]), [pl(fin)], [])
-    for o in range(O):
-        mm(5 + 2 * o, v("wq", 128 * o, 128 * o + 128), fin)
-    act(v("yb", 0, K), ps(5, 0, K), AF.Copy)
-    cp(v("yb", K, 2 * K), ps(7, 0, K))
-    dma("s", lambda: T.y[:, 0:K], v("yb", 0, K), [v("yb", 0, K)], [])
-    dma("y", lambda: T.y[:, K:2 * K], v("yb", K, 2 * K), [v("yb", K, 2 * K)], [])
+    dma("y", lambda: T.y[:, 0:K], v("yb", 0, K), [v("yb", 0, K)], [])
+    dma("s", lambda: T.y[:, K:2 * K], v("yb", K, 2 * K), [v("yb", K, 2 * K)], [])
 
     acc, edges = {}, []
     for i, r in enumerate(prog):
@@ -547,10 +564,13 @@ def rank_program(g, core, T, topo):
         for j, wait in e.items():
             succ[j].append((i, wait))
 
-    def guess(compute, product, wake, same, local, link):
+    def guess(compute, product, wake, same, local, link, big):
         cost = [r["cost"] * (product if r["q"] == "t" else 1.0 if r["kind"] != "c" else compute) for r in prog]
         lag = {"c": 0.0, "d": local, "r": link, "a": 0.0}
         gaps = [{j: (0.0 if not wait else lag[prog[j]["kind"]] + (same if prog[j]["q"] == prog[i]["q"] and prog[j]["kind"] == "c" else wake)) for j, wait in e.items()} for i, e in enumerate(preds)]
+        for i, r in enumerate(prog):
+            if r["kind"] == "a" and r["sem"][2] == "w":
+                gaps[i][r["after"][0]] += big
         return cost, lag, gaps, cost, [lag[r["kind"]] for r in prog], [[(j, d) for j, d in e.items() if d] for e in gaps]
 
     qn = {q: k for k, q in enumerate("vstgy")}

@@ -1,21 +1,30 @@
 from concourse.mybir import dt, AluOpType as OP, ActivationFunctionType as AF
 
 P, K, O = 512, 192, 2
-WA, WB, WZ, WM, WY, WE = 32, 224, 416, 448, 640, 704
-NSEM = 48
-MID = 352
+WM, WZ, WA, WB, WE = 0, 192, 256, 512, 704
+ZB = 224
+NSEM = 24
+LIFT = 1024.0
 ROUND16 = 1.5 * 2.0 ** 27
+ROUND2 = 1.5 * 2.0 ** 24
 BF, F32, I32, U16, CODE, U8 = "bfloat16", "float32", "int32", "uint16", "float8_e4m3fn_x4", "uint8"
 SCRATCH = {"ps": ("psum", [128, 4096], F32)}
 PLACE = {}
 _TOP = {}
 _ALIGN = {BF: 16, F32: 8, I32: 8, U16: 16}
-_ALONE = ("ut", "urt", "grt", "wt", "nbw", "yb", "yw0", "yw1")
+_ALONE = ("ut", "urt", "grt", "wt", "nbw", "yb", "yw0", "yw1", "kz", "ofb0", "ofb1", "off0", "off1", "msg", "lnd", "trit", "mem1")
 _CONST = []
-ORDER = {}
-TRIALS, MOVES = 60, 24000
-GUESSES = ((1.0, 1.0, 200.0, 100.0, 1500.0, 1500.0, 1200.0), (1.2, 1.2, 100.0, 50.0, 2000.0, 2000.0, 1500.0), (1.0, 0.7, 300.0, 150.0, 1300.0, 1500.0, 1000.0), (1.3, 1.4, 150.0, 50.0, 1500.0, 2000.0, 2000.0))
-BASE = (35000.0, 36000.0, 37000.0, 41000.0)
+ORDER = (
+    1, 0, 2, 15, 12, 9, 10, 6, 5, 7, 14, 20, 41, 16, 21, 17, 51, 19, 13, 11, 23, 47, 40, 3, 4, 36, 48, 49, 46, 18, 35, 33, 34, 32, 50, 53, 52, 22, 26, 8, 56, 61, 124, 55, 54, 58, 57,
+    27, 60, 59, 66, 63, 62, 71, 68, 67, 65, 64, 39, 73, 79, 75, 78, 76, 38, 70, 83, 82, 84, 72, 69, 74, 93, 80, 81, 77, 30, 92, 87, 88, 99, 98, 94, 100, 85, 101, 86, 102, 91, 95, 96,
+    89, 97, 103, 90, 122, 119, 121, 120, 123, 24, 112, 25, 126, 127, 107, 110, 105, 104, 111, 106, 113, 42, 128, 129, 45, 44, 131, 136, 118, 31, 135, 138, 43, 116, 132, 114, 130, 133,
+    134, 139, 115, 28, 140, 137, 182, 181, 141, 109, 108, 117, 29, 143, 149, 148, 150, 142, 146, 147, 145, 144, 151, 167, 152, 153, 154, 185, 187, 189, 183, 155, 37, 184, 125, 156,
+    157, 158, 186, 191, 188, 190, 192, 172, 197, 193, 195, 194, 196, 169, 159, 163, 160, 161, 170, 173, 168, 162, 198, 199, 200, 176, 174, 203, 204, 166, 165, 205, 207, 164, 201, 202,
+    209, 178, 179, 177, 175, 206, 208, 210, 211, 212, 171, 213, 180, 214, 215, 221, 220, 222, 223, 224, 216, 225, 226, 227, 230, 229, 228, 218, 232, 217, 219, 236, 233, 243, 241, 239,
+    231, 237, 235, 234, 284, 283, 245, 246, 247, 248, 249, 240, 251, 250, 258, 259, 238, 257, 253, 255, 254, 252, 260, 262, 261, 319, 318, 285, 287, 289, 291, 293, 244, 256, 288, 290,
+    263, 286, 265, 278, 264, 266, 276, 242, 292, 294, 297, 298, 295, 296, 280, 299, 300, 267, 271, 275, 268, 269, 320, 277, 279, 270, 301, 302, 305, 274, 273, 306, 307, 272, 303, 304,
+    309, 311, 308, 310, 312, 281, 315, 313, 314, 321, 316, 317, 322, 323, 282, 327, 326, 328, 329, 330, 331, 332, 334, 336, 324, 333, 335, 337, 338, 339, 340, 347, 348, 325, 341, 342,
+    343, 345, 349, 344, 346, 350, 351, 357, 353, 352, 356, 354, 355)
 
 
 def _buf(name, n, t):
@@ -37,35 +46,32 @@ def _mx(name, n):
 
 
 for _n, _w, _t in (
-        ("one", 512, BF), ("zt", 544, BF), ("i16", K, BF), ("i192", K, BF), ("i2", K, BF), ("idt", 128, BF), ("ebf", 528, BF), ("e2t", 512, BF), ("mone", 128, BF), ("tri0", 128, BF),
-        ("ni", 1, I32), ("nl", 1, I32), ("nf", 4, F32), ("nlf", 1, F32), ("nx", 4, F32), ("nrept", 1088, BF), ("dlt", 512, BF), ("trit", 1024, BF),
-        ("jx", 2, F32), ("jdt", 512, BF), ("idn", 4 * K, BF), ("zo", 8, U16),
-        ("kw", 12, F32), ("jw", 3, I32), ("jf", 3, F32), ("jwf", 3, F32), ("dl", 3, F32), ("dh0", 3, F32),
-        ("isa", 3, F32), ("nisa", 3, F32), ("basea", 3, F32), ("b511", 4, F32),
-        ("lk", K, F32), ("cn", 1, F32), ("cw", 1, F32), ("cz", 1, F32), ("cth", 1, F32)):
+        ("i16", K, BF), ("i192", K, BF), ("i2", K, BF), ("i512", P, BF), ("ebf", 515, BF), ("upp", 128, BF), ("tri0", 128, BF), ("trit", 1024, BF),
+        ("lk", K, BF), ("dg", 128, BF), ("ni", 1, I32), ("nl", 1, I32), ("nf", 4, F32), ("nlf", 1, F32), ("nx", 4, F32), ("b511", 4, F32),
+        ("vala", K, F32), ("valb", K, F32), ("cn", 1, F32), ("cm", 1, F32), ("cy", 1, F32), ("cb", 1, F32), ("cd", 1, F32)):
     _CONST.append(_n)
     _buf(_n, _w, _t)
 for _n, _w, _t in (
-        ("ut", 4, BF), ("urt", 552, BF), ("grt", 4 * P, BF), ("wt", 1024, BF),
-        ("srow", P, F32), ("scol", 4, F32), ("xd", 512, BF), ("c0t", 4 * P, BF), ("p0", 16, F32), ("junk", 10 * 128, BF), ("junk2", 4 * K, BF), ("junk3", 4 * K, BF),
-        ("x1", 4, F32), ("x2", 4, F32), ("x3", 4, F32), ("ot", 4 * K, BF), ("sc", K, F32), ("off0", 12, U16),
-        ("ordt", 4 * 384, BF), ("nnc", 3, F32), ("misc", 832, BF), ("dht", 512, BF), ("tau", 4 * K, BF), ("ct", 4 * K, BF), ("st", 4 * K, BF),
-        ("ntk", 3, F32), ("plc", 3, F32), ("nbw", K, F32), ("yb", O * K, F32), ("yw0", WY, F32), ("yw1", WY, F32)):
+        ("kz", 744, BF), ("ut", 4, BF), ("urt", 512, BF), ("grt", 4 * P, BF), ("wt", 1024, BF), ("nrept", 1024, BF),
+        ("srow", P, F32), ("scol", 4, F32), ("xd", 512, BF), ("c0t", 4 * P, BF), ("p0", 16, F32), ("junk", 10 * 128, BF),
+        ("x1", 4, F32), ("x2", 4, F32), ("x3", 4, F32), ("ot", 4 * K, BF), ("inv0", P, F32), ("mem0", P, BF), ("mem1", P, BF), ("scy", P, F32), ("offy", 32, U16),
+        ("hi", 3, F32), ("lo", 3, F32), ("msg", 6, U16), ("lnd", 6, U16), ("offc", 12, U16), ("off2", 12, U16), ("sc2", K, F32),
+        ("ntk", 3, F32), ("nbw", K, F32), ("yb", O * K, F32), ("yw0", 2 * K, F32), ("yw1", 2 * K, F32)):
     _buf(_n, _w, _t)
-for _n, _w in (("ur", 128), ("uq", 136), ("q0", P), ("wq", 256), ("oneq", 128), ("zq", 128), ("nrep", 256), ("dlq", 128), ("eq", 640), ("triq", 256),
-               ("jdq", 128), ("idq", K), ("ndcq", 144), ("c0q", P), ("oh", 320), ("ordq", 384), ("xq", 128), ("rep", 128), ("repb", 128), ("fin", K)):
+for _n, _a, _w in (("nd", 0, 520), ("ft1", 12, 512), ("ft0", 16, 512), ("one", 20, 512), ("xt", 212, 512), ("zt", 216, 528)):
+    PLACE[_n] = ("kz", _a, _w)
+for _n, _w in (("ur", 128), ("q0", P), ("wq", 256), ("oneq", 128), ("nrep", 256), ("eq", 512), ("triq", 256), ("c0q", P), ("oh", K),
+               ("drq", 256), ("dy", P), ("ndq", 130), ("xq", 128), ("fw", 2 * K), ("fin", K)):
     _mx(_n, _w)
 for _s in "01":
     for _n, _w, _t in (
-            ("na", 3, F32), ("nc", 3, F32), ("nr", 384, BF), ("mt", 4 * K, BF), ("scb", K, F32), ("off1", 12, U16), ("offb", 12, U16), ("ub", 12, F32), ("ub2", 12, F32),
-            ("bor", K, BF), ("keep", 2, F32), ("fm", 2, F32), ("dhr", 2, F32), ("du", 2, F32), ("fo", 3, F32), ("bi", 2, F32),
-            ("ht", 4 * K, BF), ("arow", K, F32), ("acol", 3, F32), ("v", 3 * K, BF), ("rs", 3, F32), ("bs", 3, F32), ("rf", 3, F32),
-            ("scs", K, F32), ("offs", 12, U16)):
+            ("sc", K, F32), ("off", 12, U16), ("ofb", 12, U16), ("nr", 2 * K, BF), ("bor", K, BF), ("val", K, F32), ("scv", K, F32), ("offn", 12, U16),
+            ("scd", 2 * K, F32), ("nnc", 3, F32), ("par", 3, F32), ("even", 3, F32), ("ht", 4 * K, BF), ("arow", K, F32), ("acol", 3, F32), ("v", 3 * K, BF), ("acc", 3, F32)):
         _buf(_n + _s, _w, _t)
-    for _n, _w in (("nbq", 128), ("tl", 128), ("mtq", 256), ("win", WE), ("an", K), ("bp", K), ("ftq", 136), ("dhq", 128), ("tauq", K), ("ndq", 136), ("cq", 256), ("sq", 320)):
+    for _n, _w in (("win", WE), ("ap", K), ("bn", 256), ("ftq", 128), ("cq", 2 * K if _s == "0" else 3 * K), ("sq", K)):
         _mx(_n + _s, _w)
-ARR = ["tc0", "ts0", "wc0", "ws0", "tc1", "ts1", "wc1", "ws1"]
-SEMAPHORES = ["q_v", "q_s", "q_t", "q_g"] + ["d%d" % i for i in range(NSEM)] + ["l_" + a for a in ARR] + ["a_" + a for a in ARR]
+ARR = ["ls0", "wc0", "ws0", "ls1", "wc1", "ws1"]
+SEMAPHORES = ["q_v", "q_s", "q_t", "q_g", "out"] + ["d%d" % i for i in range(NSEM)] + ["l_" + a for a in ARR] + ["a_" + a for a in ARR]
 
 
 def rank_program(g, core, T, topo):
@@ -80,6 +86,9 @@ def rank_program(g, core, T, topo):
             return (name, a, b, s, p, e, cast)
         home, o, n = PLACE[name]
         return (home, o + a, o + (n if b is None else b), s, p, e, cast)
+
+    low = lambda x: x[:4] + (0, 64) + x[6:]
+    high = lambda x: x[:4] + (64, 128) + x[6:]
 
     def ap(x):
         if not isinstance(x, tuple):
@@ -98,48 +107,40 @@ def rank_program(g, core, T, topo):
         if x[0] == "ps":
             f = lambda r: set(c // 512 for c in range(r[1], r[2], r[3] if r[3] == 512 else 1))
             return bool(f(x) & f(y))
-        if x[1] >= y[2] or y[1] >= x[2]:
+        if x[1] >= y[2] or y[1] >= x[2] or x[4] >= y[5] or y[4] >= x[5]:
             return False
         if x[3] == y[3] and x[3] > 1:
             return (x[1] - y[1]) % x[3] == 0
         return True
 
-    def rec(q, fn, reads, writes, cost, kind="c", sem=None, amount=0, after=()):
-        prog.append({"q": q, "fn": fn, "reads": reads, "writes": writes, "cost": cost, "kind": kind, "sem": sem, "amount": amount, "after": list(after)})
+    def rec(q, fn, reads, writes, kind="c", sem=None, amount=0, after=()):
+        prog.append({"q": q, "fn": fn, "reads": reads, "writes": writes, "kind": kind, "sem": sem, "amount": amount, "after": list(after)})
         return len(prog) - 1
 
     tens = lambda *xs: [x for x in xs if isinstance(x, tuple)]
-    short = lambda x: x[0][1:] in (BF, U16) or x[0] in ("ut", "urt", "grt", "wt")
-
-    def easy(*xs):
-        return 0.83 * max(64, width(xs[0]) * (0.5 if all(short(x) for x in xs) else 1))
 
     def ts(out, in0, s1, op0, s2=None, op1=None):
         if op1 is None:
             fn = lambda: g.vector.tensor_scalar(out=ap(out), in0=ap(in0), scalar1=ap(s1), scalar2=None, op0=op0)
         else:
             fn = lambda: g.vector.tensor_scalar(out=ap(out), in0=ap(in0), scalar1=ap(s1), scalar2=ap(s2), op0=op0, op1=op1)
-        return rec("v", fn, tens(in0, s1, s2), [out], easy(out, in0))
+        return rec("v", fn, tens(in0, s1, s2), [out])
 
-    def tt(out, a, b, op):
-        f = 1 if "ps" in (a[0], b[0]) else 2
-        rec("v", lambda: g.vector.tensor_tensor(out=ap(out), in0=ap(a), in1=ap(b), op=op), [a, b], [out], 0.83 * max(64, f * width(out)))
+    def tt(out, a, b, op, off=None):
+        rec("v", lambda: g.vector.tensor_tensor(out=ap(out), in0=ap(a).indirect(ap(off)) if off else ap(a), in1=ap(b), op=op), tens(a, b, off), [out])
 
     def cp(out, a):
-        rec("v", lambda: g.vector.tensor_copy(ap(out), ap(a)), [a], [out], easy(out, a))
+        rec("v", lambda: g.vector.tensor_copy(ap(out), ap(a)), [a], [out])
 
     def fill(out, c=0.0):
-        rec("v", lambda: g.vector.memset(ap(out), c), [], [out], easy(out))
+        rec("v", lambda: g.vector.memset(ap(out), c), [], [out])
 
-    def act(out, a, func, bias=None, scale=None, accum=None):
-        kw = {}
-        if bias is not None:
-            kw["bias"] = bias
-        if scale is not None:
-            kw["scale"] = scale
-        if accum is not None:
-            kw["accum_out"] = accum
-        rec("s", lambda: g.scalar.activation(ap(out), ap(a), func, **{k: ap(x) for k, x in kw.items()}), tens(a, bias, scale), tens(out, accum), 0.83 * max(64, width(out)) + (20 if accum else 0))
+    def scan(out, lift, row):
+        rec("v", lambda: g.vector.tensor_tensor_scan(ap(out), ap(lift), ap(row), 0.0, OP.add, OP.max), [lift, row], [out])
+
+    def act(out, a, func, bias=None, scale=None, accum=None, off=None):
+        kw = {k: x for k, x in (("bias", bias), ("scale", scale), ("accum_out", accum)) if x is not None}
+        rec("s", lambda: g.scalar.activation(ap(out), ap(a).indirect(ap(off)) if off else ap(a), func, **{k: ap(x) for k, x in kw.items()}), tens(a, bias, scale, off), tens(out, accum))
 
     def zero(out):
         act(out, v("zt", 0, width(out)), AF.Copy)
@@ -147,49 +148,49 @@ def rank_program(g, core, T, topo):
     def pl(x):
         return (x[0] + "s",) + x[1:6] + (None,)
 
-    def quant(out, a):
-        return rec("v", lambda: g.vector.quantize_mx(ap(out), ap(pl(out)), ap(a)), [a], [out, pl(out)], 12 + 0.22 * width(a))
+    def quant(out, a, after=()):
+        return rec("v", lambda: g.vector.quantize_mx(ap(out), ap(pl(out)), ap(a)), [a], [out, pl(out)], after=after)
 
     def mm(bank, l, r, start=True, stop=True):
         out = v("ps", 512 * bank, 512 * bank + width(r))
-        rec("t", lambda: g.tensor.matmul_mx(ap(out), ap(l), ap(pl(l)), ap(r), ap(pl(r)), start, stop), [l, pl(l), r, pl(r)], [out], 1.2 * (width(r) + 16))
+        rec("t", lambda: g.tensor.matmul_mx(ap(out), ap(l), ap(pl(l)), ap(r), ap(pl(r)), start, stop), [l, pl(l), r, pl(r)], [out])
 
-    def gather(q, out, win, off, c=lambda x: x):
-        n = 1.3 * width(out)
-        if q == "v":
-            rec("v", lambda: g.vector.tensor_copy(ap(c(out)), ap(c(win)).indirect(ap(off))), [win, off], [out], 50 + n)
-        else:
-            rec("s", lambda: g.scalar.activation(ap(out), ap(win).indirect(ap(off)), AF.Copy), [win, off], [out], 65 + n)
+    def gather(out, win, off, c=lambda x: x):
+        rec("v", lambda: g.vector.tensor_copy(ap(c(out)), ap(c(win)).indirect(ap(off))), [win, off], [out])
+
+    def scatter(win, off, a):
+        rec("v", lambda: g.vector.tensor_copy(ap(win).indirect(ap(off)), ap(a)), [a, off, win], [win])
 
     def pick(out, win, off):
-        gather("v", out, win, off, lambda x: x[:6] + (32,))
-        gather("s", pl(out), pl(win), off)
+        gather(out, win, off, lambda x: x[:6] + (32,))
+        act(pl(out), pl(win), AF.Copy, off=off)
 
-    def dma(q, out, in_, reads, writes, after=()):
-        n = nd[0]
-        nd[0] += 1
-        rec(q, lambda: ENG[q].dma_start(out() if not isinstance(out, tuple) else ap(out), in_() if not isinstance(in_, tuple) else ap(in_)), reads, writes, 60, "d", "d%d" % n, 16, after)
+    def dma(q, out, in_, reads, writes, after=(), store=False):
+        sem = "out" if store else "d%d" % nd[0]
+        nd[0] += not store
+        rec(q, lambda: ENG[q].dma_start(out() if not isinstance(out, tuple) else ap(out), in_() if not isinstance(in_, tuple) else ap(in_)), reads, writes, "d", sem, 16, after)
 
     def mxcopy(q, out, in_, after=()):
         c = lambda x: x[:6] + (8,)
         dma(q, c(out), c(in_), [in_], [out], after)
         dma(q, pl(out), pl(in_), [pl(in_)], [pl(out)], after)
 
-    def send(peer, out, in_, key):
+    def send(peer, out, in_, key, after=()):
         dst = T.cores[peer]
         rid, pid, _ = topo.addr(dst)
         m, n = topo.mask(core, dst), len(topo.engines(core, dst))
-        i = rec("g", lambda: g.remote_dma(ap(out), ap(in_), T.sem["a_" + key], T.sem["l_" + key], pid, rid, m), [in_], [], 120, "r", "l_" + key, n)
+        i = rec("g", lambda: g.remote_dma(ap(out), ap(in_), T.sem["a_" + key], T.sem["l_" + key], pid, rid, m), [in_], [], "r", "l_" + key, n, after)
         sent[key] = (i, out, len(topo.engines(dst, core)))
+        return i
 
-    def sendmx(peer, out, in_, kc, ks):
+    def sendmx(peer, out, in_, kc, ks, after=()):
         c = lambda x: x[:6] + (8,)
-        send(peer, c(out), c(in_), kc)
-        send(peer, pl(out), pl(in_), ks)
+        send(peer, c(out), c(in_), kc, after)
+        send(peer, pl(out), pl(in_), ks, after)
 
     def arrive(key):
         i, out, n = sent[key]
-        rec(None, None, [], [out], 0, "a", "a_" + key, n, [i])
+        return rec(None, None, [], [out], "a", "a_" + key, n, [i])
 
     ps = lambda bank, a, b, s=1: v("ps", 512 * bank + a, 512 * bank + b, s)
     pst = lambda bank, n, c: v("ps", 512 * bank + c, 512 * (bank + n - 1) + c + 1, 512)
@@ -198,30 +199,27 @@ def rank_program(g, core, T, topo):
 
     def iota(out, pattern, base, cm, flag=True):
         kw = {"allow_small_or_imprecise_dtypes": True} if flag else {}
-        rec("g", lambda: g.iota(ap(out), pattern, base, cm, **kw), [], [out], 130 + 1.66 * width(out))
+        rec("g", lambda: g.iota(ap(out), pattern, base, cm, **kw), [], [out])
 
     def select(out, in_, pattern, op, fillv, base, cm):
-        rec("g", lambda: g.affine_select(ap(out), ap(in_), pattern, op, fillv, base, cm), [in_], [out], 170 + 1.66 * width(out))
+        rec("g", lambda: g.affine_select(ap(out), ap(in_), pattern, op, fillv, base, cm), [in_], [out])
 
     dma("y", v("ut"), lambda: T.u[:, 0:4], [], [v("ut")])
     for c in range(4):
         x = v("grt", 512 * c, 512 * c + 512)
         dma("sy"[c % 2], x, (lambda c=c: T.gr[:, 512 * c:512 * c + 512]), [], [x])
 
-    fill(v("one"), 1.0)
-    fill(v("zt"))
-    fill(v("zo"), 0)
-    select(v("idt"), one, [[-1, 128]], OP.is_equal, 0.0, 0, 1)
-    fill(v("mone"), -0.5)
-    select(v("tri0"), v("mone"), [[1, 128]], OP.is_gt, 2.0, 0, -1)
+    fill(v("kz", 0, 212), 1.0)
+    fill(v("kz", 212, 744))
+    select(v("upp"), one, [[1, 128]], OP.is_gt, 0.0, 0, -1)
+    ts(v("tri0"), v("upp"), -1.0, OP.mult, 0.5, OP.add)
     iota(v("ni"), [[0, 1]], 0, 1, False)
     iota(v("nf"), [[128, 4]], -256, 1)
     iota(v("b511"), [[-128, 4]], 511, -1)
     iota(v("i16"), [[0, 12], [1, 16]], 0, 0)
     iota(v("i192"), [[1, K]], 0, 0)
-    iota(v("jf"), [[128, 3]], 0, 1)
-    iota(v("jw"), [[128, 3]], 16, 1, False)
-    iota(v("kw"), [[16, 12]], WA, 0)
+    iota(v("i512"), [[1, P]], -256, 0)
+    iota(v("cd"), [[0, 1]], 127 * int(LIFT), -int(LIFT))
     ts(v("nl"), v("ni"), 15, OP.bitwise_and)
     cp(v("nlf"), v("nl"))
     nlf = v("nlf")
@@ -231,74 +229,38 @@ def rank_program(g, core, T, topo):
     fill(v("p0"))
     quant(v("oneq"), v("one"))
     ts(v("lk"), v("i16"), nlf, OP.is_equal, -1.0e6, OP.mult)
-    act(v("lk"), v("lk"), AF.Copy, bias=4096.0)
-    lift = lambda out, c, f=1.0: act(out, nlf, AF.Copy, scale=4096.0 * f, bias=c - 4096.0 * 15 * f)
-    lift(v("cn"), 256.0)
-    lift(v("cw"), float(MID))
-    lift(v("cz"), float(K))
-    lift(v("cth"), -0.5, -1.0)
-    ts(v("kw"), v("kw"), nlf, OP.add)
-    ts(v("jw"), v("jw"), 31, OP.bitwise_and)
-    cp(v("jwf"), v("jw"))
-    act(v("dl"), v("jwf"), AF.Copy, bias=-16.0)
-    tt(v("dh0"), v("jf"), v("jwf"), OP.subtract)
-    act(v("dh0"), v("dh0"), AF.Copy, bias=16.0 + WA - MID)
-    ts(v("isa"), v("jf"), K - 0.5, OP.is_gt)
-    act(v("nisa"), v("isa"), AF.Copy, scale=-1.0)
-    tt(v("basea"), v("jf"), v("isa"), OP.mult)
-    select(v("trit", 1, 1024, 4), v("one", 0, 256), [[1, 256]], OP.is_gt, 0.0, 0, -1)
-    select(v("trit", 2, 1024, 4), v("one", 0, 256), [[1, 256]], OP.is_gt, 0.0, -128, -1)
-    select(v("trit", 1, 1024, 4), v("trit", 1, 1024, 4), [[1, 256]], OP.not_equal, -960.0, 0, -1)
-    select(v("trit", 2, 1024, 4), v("trit", 2, 1024, 4), [[1, 256]], OP.not_equal, -960.0, -128, -1)
-    zero(v("trit", 0, 1024, 4))
-    zero(v("trit", 3, 1024, 4))
-    fill(v("ebf"))
-    act(v("ebf", 8, 520, 4), v("idt"), AF.Copy)
-    select(v("e2t"), v("ebf", 8, 520), [[1, 512]], OP.not_equal, 1.0, -2, -4)
+    act(v("lk"), v("lk"), AF.Copy, bias=LIFT)
+    lift = lambda out, c, f: act(out, nlf, AF.Copy, scale=LIFT * f, bias=c - LIFT * 15 * f)
+    lift(v("cn"), 256.0, 1.0)
+    lift(v("cm"), 256.0, -1.0)
+    lift(v("cy"), 0.0, -512.0)
+    lift(v("cb"), -float(ZB), -512.0)
+    select(v("ebf"), v("zt", 0, 515), [[1, 515]], OP.not_equal, -0.5, -3, -4)
+    ts(v("dg"), v("ebf", 3, 515, 4), 2.0e6, OP.mult, LIFT, OP.add)
     for t in range(4):
-        act(v("nrept", 64 + t, 576, 4), one, AF.Identity, scale=v("nx", t, t + 1))
-    act(v("nrept", 576, 1088), v("one"), AF.Identity, scale=nlf)
-    fill(v("nrept", 0, 64))
-    for c in (1, 4):
-        act(v("nrept", 4 * c, 4 * c + 4), v("nx"), AF.Copy)
-        act(v("nrept", 4 * c + 8, 4 * c + 12), v("one", 0, 4), AF.Identity, scale=nlf)
-    act(v("nrept", 48, 49), v("isa", 1, 2), AF.Copy)
-    act(v("nrept", 49, 50), v("one", 0, 1), AF.Copy)
-    zero(v("dlt", 3, 512, 4))
-    for t in range(3):
-        act(v("dlt", t, 512, 4), one, AF.Identity, scale=v("dl", t, t + 1))
-    tt(v("jx", 0, 1), v("nx", 0, 1), v("isa", 1, 2), OP.mult)
-    tt(v("jx", 1, 2), nlf, v("isa", 1, 2), OP.mult)
-    for e, x in enumerate((v("jx", 0, 1), v("nx", 1, 2), v("jx", 1, 2), nlf)):
-        act(v("jdt", e, 512, 4), one, AF.Identity, scale=x)
-    for e in range(2):
-        select(v("idn", e, 4 * K, 4), v("one", 0, K), [[1, K]], OP.is_equal, 0.0, 64 - 128 * e, -1)
-        act(v("idn", 2 + e, 4 * K, 4), v("idn", e, 4 * K, 4), AF.Copy)
-    for k in range(2):
-        zero(v("misc", 416 * k, 416 * k + 416))
-    zero(v("urt", 0, 40))
-    for name, a, b, st in (("dht", 3, 512, 4), ("tau", 3, 4 * K, 4), ("st", 3, 4 * K, 4), ("ct", 3, 4 * K, 4), ("ordt", 3, 4 * 384, 4), ("rf1", 0, 1, 1), ("na0", 2, 3, 1), ("na1", 2, 3, 1),
-                           ("yw0", 0, WA, 1), ("yw0", WZ, WM, 1), ("yw1", 0, WA, 1), ("yw1", WZ, WM, 1)):
-        zero(v(name, a, b, st))
-    act(v("dht", 2, 512, 4), one, AF.Identity, scale=v("dh0", 2, 3))
+        act(v("nrept", t, 512, 4), one, AF.Identity, scale=v("nx", t, t + 1))
+    act(v("nrept", 512, 1024), v("zt", 0, 512), AF.Identity, bias=nlf)
     act(v("i2"), v("i192"), AF.Copy, scale=2.0, bias=1.0 - K)
-    quant(v("zq"), v("zt", 0, 512))
+    act(v("vala"), v("i192"), AF.Copy, scale=-1.0 / 512, bias=-WA / 512.0)
+    act(v("valb"), v("i192"), AF.Copy, scale=1.0 / 512, bias=WB / 512.0)
+    zero(v("inv0"))
+    zeros = quant(v("win0", 128, 256), v("zt", 0, 512))
     for b in range(4):
-        quant(v("eq", 128 * b, 128 * b + 128), v("ebf", 8 - b, 520 - b))
-    quant(v("eq", 512, 640), v("e2t"))
+        quant(eb(b), v("ebf", 3 - b, 515 - b))
 
     for t in range(4):
         if t < 2:
-            ts(v("urt", 40 + t, 552, 4), one, v("ut", t, t + 1), OP.mult)
+            ts(v("urt", t, 512, 4), one, v("ut", t, t + 1), OP.mult)
         else:
-            act(v("urt", 40 + t, 552, 4), v("zt", 0, 128), AF.Identity, bias=v("ut", t, t + 1))
-    quant(v("ur"), v("urt", 40, 552))
+            act(v("urt", t, 512, 4), v("zt", 0, 128), AF.Identity, bias=v("ut", t, t + 1))
+    quant(v("ur"), v("urt"))
+    ur = v("ur")
 
     def sizes(c):
         qc = v("q0", 128 * c, 128 * c + 128)
-        i = quant(qc, v("grt", 512 * c, 512 * c + 512))
-        mm(4 + c % 3, qc, v("ur"))
-        mm(c, v("ur"), qc)
+        i = quant(qc, v("grt", 512 * c, 512 * c + 512), [zeros] if c == 3 else [])
+        mm(4 + c % 3, qc, ur)
+        mm(c, ur, qc)
         act(v("scol", c, c + 1), ps(4 + c % 3, 0, 1), AF.Abs)
         act(v("srow", 128 * c, 128 * c + 128), ps(c, 0, 128), AF.Abs)
         return i
@@ -318,7 +280,7 @@ def rank_program(g, core, T, topo):
                 ts(blk, row, v("scol", t, t + 1), OP.is_le)
 
     def count(c):
-        for t in range(c + 1) if c else ():
+        for t in range(min(c + 1, 3)) if c else ():
             k = c * (c + 1) // 2 + t
             d = 128 if k == 1 else 0
             act(v("junk", 128 * k - d, 128 * k + 128), v("c0t", 512 * c + t - 4 * d, 512 * c + 512, 4), AF.Copy, accum=v("p0", 4 * c + t, 4 * c + t + 1))
@@ -332,217 +294,190 @@ def rank_program(g, core, T, topo):
         compare(c)
     for c in range(4):
         count(c)
+    dma("y", v("wt"), lambda: T.w[:, :], [], [v("wt")], [early[3]])
+    for name in ("win1", "bn0", "bn1"):
+        mxcopy("y", v(name, WZ, WA), v("win0", WZ, WA), [early[3]])
+    for x in (v("trit", 0, 512), v("trit", 512, 1024), v("mem1")):
+        dma("y", x, v("zt", 0, 512), [v("zt", 0, 512)], [x], [early[3]])
+    select(v("trit", 514, 1024, 4), v("upp"), [[1, 128]], OP.not_equal, -960.0, 0, -1)
+    act(high(v("trit", 1, 512, 4)), high(v("trit", 514, 1024, 4)), AF.Copy)
+    act(high(v("trit", 513, 1024, 4)), high(one), AF.Copy)
+    quant(v("triq"), v("trit"))
+    quant(v("wq"), v("wt"))
 
-    def listof(bank, digits, onehot, scan, off, shift):
-        for k, d in enumerate(digits):
-            mm(bank, d, onehot, k == 0, k == len(digits) - 1)
-        row = ps(bank, 0, K)
-        rec("v", lambda: g.vector.tensor_tensor_scan(ap(scan), ap(v("lk")), ap(row), 0.0, OP.add, OP.max), [v("lk"), row], [scan], 0.83 * K)
-        last = (scan[0], scan[1] + 15, scan[2], 16) + scan[4:]
-        ts(off, last, shift, OP.add)
-        return last
+    def listof(bank, digits, onehot, sc):
+        for k in range(2):
+            mm(bank, v(digits, 128 * k, 128 * k + 128), onehot, k == 0, k == 1)
+        scan(v(sc), v("lk"), ps(bank, 0, K))
+        return v(sc, 15, K, 16)
 
-    for t in range(4):
-        ts(v("ot", t, 4 * K, 4), v("i192"), ps(t, 0, 1), OP.subtract, v("x3", t, t + 1), OP.is_equal)
-    quant(v("oh", 64, 256), v("ot"))
-    for name, after in (("oh", early[0]), ("sq0", early[3])):
-        mxcopy("y", v(name, 0, 64), v("zq", 0, 64), [after])
-        mxcopy("y", v(name, 256, 320), v("zq", 0, 64), [after])
-    quant(v("nrep"), v("nrept", 64, 1088))
-    quant(v("ndcq"), v("nrept", 0, 576))
-    quant(v("idq"), v("idn"))
-    quant(v("jdq"), v("jdt"))
+    st = lambda t: v("ot", t, 4 * K, 4)
+    for t in range(3):
+        ts(st(t), v("i192"), ps(t, 0, 1), OP.subtract, v("x3", t, t + 1), OP.is_equal)
+    ts(st(3), v("i192"), ps(3, 0, 1), OP.is_equal)
+    quant(v("oh"), v("ot"))
+    quant(v("nrep"), v("nrept"))
+    zero(st(3))
 
-    zone = {name: 48 * (6 - k) for k, name in enumerate(("nbt0", "ft0", "ndt0", "nbt1", "ft1", "ndt1", "xt"))}
-    mi = lambda name, a, b: v("misc", zone[name] + a, zone[name] + b)
+    ct = lambda t: v("c0t", t, 4 * K, 4)
+    ordb = lambda t: v("c0t", 4 * K + t, 8 * K, 4)
+    orda = lambda t: v("junk", t, 4 * K, 4)
 
-    def describe(s, peer, oh, digits):
-        hi, lo = v(digits, 4, 132), v(digits, 0, 128)
-        mm(4, v(oh, 0, 128), hi, True, False)
-        mm(4, v(oh, 128, 256), lo, False, True)
-        cp(mi("nbt" + s, 0, 8), ps(4, 0, 8))
-        i = quant(v("nbq" + s), mi("nbt" + s, 0, 512))
-        sendmx(peer, v("tl" + s, 0, 8), v("nbq" + s, 0, 8), "tc" + s, "ts" + s)
-        mm(5, v(oh, 64, 192), hi, True, False)
-        mm(5, v(oh, 192, 320), lo, False, True)
-        ts(v("nc" + s, 0, 1), ps(5, 0, 1), ps(5, 2, 3), OP.add)
-        ts(v("na" + s, 1, 2), ps(5, 1, 2), ps(5, 3, 4), OP.add)
-        if s == "1":
-            pick(v("rep"), v("nbq" + s), v("zo"))
-            mm(7, v("rep"), v("idq"))
-            act(v("nr" + s, 0, K), ps(7, 0, K), AF.Copy)
-        return i
-
-    def own(s):
-        for b in range(4):
-            mm(b, eb(b), v("win" + s, WA, WB), True, False)
-
-    def before(s, last):
+    def give(s, peer, table, first):
         w = "win" + s
-        arrive("tc" + s)
-        arrive("ts" + s)
-        mm(4, eb(4), v("tl" + s))
-        for e in range(4):
-            ts(v("mt" + s, e, 4 * K, 4), v("nr" + s, 0, K), ps(4, e % 2, e % 2 + 1), OP.is_equal)
-        quant(v("mtq" + s, 0, K), v("mt" + s))
-        scan = listof(7, (v("jdq"),), v("mtq" + s, 0, K), v("scb" + s), v("off1" + s), v("cz"))
-        act(v("bor" + s), ps(7, 0, K), AF.Sign, scale=-1.0)
-        ts(v("ub" + s), scan, v("cth"), OP.is_gt)
-        tt(v("ub2" + s), v("ub" + s), v("kw"), OP.mult)
-        cp(v("offb" + s), v("ub2" + s))
-        pick(v("an" + s), v(w, 0, WB), v("offb" + s))
-        tt(v("nc" + s, 1, 3), v("na" + s, 1, 3), ps(4, 0, 2), OP.add)
-        mm(5, v("mtq" + s, 0, 128), v("ndcq", 12, 140), True, False)
-        mm(5, v("mtq" + s, 128, 256), v("ndcq", 10, 138), False, True)
-        both = ps(5, 0, 3, 2)
-        ts(v("keep" + s), both, -1.0, OP.mult, 1.0, OP.add)
-        ts(v("fm" + s), both, float(WM - WA), OP.mult)
-        tt(v("dhr" + s), v("fm" + s), v("dh0", 0, 2), OP.add)
+        pick(v(w, WA, WA + K), v(table), v("off" + s))
+        sendmx(peer, v(w, WB, WE), v(w, WA, WA + K), "wc" + s, "ws" + s, [first])
+        act(v("nr" + s, K, 2 * K), ps(6, 0, K), AF.Copy, scale=-1.0 if s == "1" else 1.0)
+        if s == "0":
+            scatter(v("inv0"), v("off0"), v("vala"))
+            act(v("mem0"), v("inv0"), AF.Sign, scale=-1.0)
+        else:
+            scatter(v("mem1"), v("off1"), v("one", 0, K))
+        scan(v("scd" + s, 256, 384), v("dg"), v("nr" + s, 256, 384))
+        mm(4, v(w, WA + 64, WA + K), ur)
+        act(v("acol" + s, 2, 3), ps(4, 0, 1), AF.Abs)
+
+    def before(s, table):
+        ofb = v("ofb" + s)
+        pick(v("ap" + s), v(table), ofb)
+        for b in range(4):
+            mm(b, eb(b), v("ap" + s), True, False)
+        act(v("bor" + s), v("mem" + s), AF.Copy, scale=-2.0, off=ofb)
+        act(v("nr" + s, 0, K), v("i512"), AF.Copy, off=ofb)
+        tt(v("val" + s), v("mem" + s), v("valb"), OP.subtract, ofb)
+        scan(v("scv" + s), v("lk"), v("val" + s))
+        ts(v("offn" + s), v("scv" + s, 15, K, 16), -512.0, OP.mult, v("cb"), OP.add)
         for t in range(2):
-            act(v("dht", t, 512, 4), one, AF.Identity, scale=v("dhr" + s, t, t + 1))
-            k = 2 * int(s) + t
-            act(v("junk3", K * k, K * k + K), v("mt" + s, t, 4 * K, 4), AF.Copy, accum=v("du" + s, t, t + 1))
-        quant(v("dhq" + s), v("dht"))
-        tt(mi("ft" + s, 9, 11), v("du" + s), v("isa", 1, 3), OP.mult)
-        ts(v("fo" + s), mi("ft" + s, 8, 11), 2.0, OP.mult, -0.5, OP.add)
-        quant(v("ftq" + s), mi("ft" + s, 0, 544))
-        mm(6, v("triq", 0, 128), v("ftq" + s, 2, 130), True, False)
-        mm(6, v("triq", 128, 256), v("ftq" + s, 0, 128), False, True)
-        tt(v("bs" + s, 1, 3), v("basea", 1, 3), ps(6, 0, 3, 2), OP.subtract)
+            scan(v("scd" + s, 128 * t, 128 * t + 128), v("dg"), v("nr" + s, 128 * t, 128 * t + 128))
+        act(v("nnc" + s), v("scd" + s, 127, 384, 128), AF.Identity, scale=-1.0, bias=v("cd"))
+        for t in (1, 2, 0):
+            act(ordb(t), v("nr" + s, 0, K), AF.Sign, bias=v("nnc" + s, t, t + 1), accum=v("par" + s, t, t + 1) if t else None)
+        ts(v("even" + s, 1, 3), v("par" + s, 1, 3), ROUND2, OP.add, -ROUND2, OP.add)
+        tt(high(v("ft" + s, 1, 2)), high(v("par" + s, 1, 2)), high(v("even" + s, 1, 2)), OP.is_equal)
+        tt(v("ft" + s, 2, 3), v("par" + s, 2, 3), v("even" + s, 2, 3), OP.is_equal)
+        quant(v("ftq" + s), v("ft" + s))
+        quant(v("cq" + s, K, 2 * K), v("c0t", 4 * K, 8 * K))
         for t in range(3):
-            ts(v("tau", t, 4 * K, 4), v("nr" + s, 0, K), v("nc" + s, t, t + 1), OP.is_le, v("fo" + s, t, t + 1), OP.add)
-        quant(v("tauq" + s), v("tau"))
-        n = mi("ndt" + s, 4, 7)
-        ts(n, v("nc" + s), ROUND16, OP.add, -ROUND16, OP.add)
-        tt(mi("ndt" + s, 12, 15), v("nc" + s), n, OP.subtract)
-        act(mi("ndt" + s, 16, 19), n, AF.Copy)
-        act(mi("ndt" + s, 24, 27), mi("ndt" + s, 12, 15), AF.Copy)
-        quant(v("ndq" + s), mi("ndt" + s, 0, 544))
-        if last:
-            pick(v("repb"), v("tl" + s), v("zo"))
-            mm(6, v("repb"), v("idq"))
-            act(v("nr" + s, K, 2 * K), ps(6, 0, K), AF.Copy)
-            ts(v("nnc"), v("nc" + s), -1.0, OP.mult)
-            for t in range(3):
-                act(v("ordt", t, 4 * 384, 4), v("nr" + s), AF.Sign, bias=v("nnc", t, t + 1))
-            quant(v("ordq"), v("ordt"))
-        for t in (1, 2):
-            mm(4 + t, eb(t), v("tauq" + s))
+            mm(4 + t, eb(t), v("cq" + s, K, 2 * K))
 
     def merge(s):
-        w, bp, an = "win" + s, "bp" + s, "an" + s
-        arrive("wc" + s)
-        arrive("ws" + s)
-        for t in range(3):
-            mm(4, v(w, WA + 128 * t, WA + 128 * t + 128), v("uq", 4 - 2 * t, 132 - 2 * t), t == 0, t == 2)
-        tt(v("bi" + s), ps(4, 0, 3, 2), v("keep" + s), OP.mult)
-        act(v("acol" + s, 2, 3), ps(4, 4, 5), AF.Abs)
-        mm(4, eb(0), v("tauq" + s))
-        pick(v(bp), v(w, WB, WM), v("off1" + s))
+        w, bn = "win" + s, "bn" + s
+        here = [arrive("wc" + s), arrive("ws" + s)]
+        pick(v(bn, 0, K), v(w, ZB, WE), v("offn" + s))
         for b in range(4):
-            mm(b, eb(b), v(bp), False, True)
+            mm(b, eb(b), v(w, WB, WE), False, True)
             tt(v("ht" + s, b, 4 * K, 4), ps(b, 0, K), v("bor" + s), OP.mult)
+        mm(7, ur, v(bn, 0, K), True, False)
+        mm(0, v(bn, 0, 128), ur, True, False)
+        mm(1, v(bn, 128, 256), ur, True, False)
+        mm(1, v(w, WZ, WZ + 128), ur, False, False)
         quant(v(w, WM, WM + K), v("ht" + s))
-        ur = v("ur")
-        mm(7, ur, v(an), True, False)
         mm(7, ur, v(w, WM, WM + K), False, True)
+        mm(0, v(w, WM, WM + 128), ur, False, True)
+        mm(1, v(w, WM + 128, WM + 256), ur, False, True)
         for t in range(2):
-            mm(0, v(w, WM + 128 * t, WM + 128 * t + 128), v("uq", 4 - 2 * t, 132 - 2 * t), t == 0, t == 1)
+            mm(2 + t, v("triq", 128 * t, 128 * t + 128), v("ftq" + s))
         act(v("arow" + s), ps(7, 0, K), AF.Abs)
-        for t in range(2):
-            act(v("acol" + s, t, t + 1), ps(0, 2 * t, 2 * t + 1), AF.Abs, bias=v("bi" + s, t, t + 1))
-        for t in (2, 0, 1):
+        act(v("acol" + s, 0, 2), pst(0, 2, 0), AF.Abs)
+        for t in (2, 1, 0):
             x = v("v" + s, K * t, K * t + K)
             act(x, v("arow" + s), AF.Sign, bias=v("acol" + s, t, t + 1), scale=-1.0)
-            tt(v("ct", t, 4 * K, 4), x, ps(4 + t, 0, K), OP.is_gt)
+            tt(ct(t), x, ps(4 + t, 0, K), OP.is_gt)
         for t in (2, 1):
-            k = 2 * int(s) + t - 1
-            act(v("junk2", K * k, K * k + K), v("ct", t, 4 * K, 4), AF.Identity, scale=v("nisa", t, t + 1), accum=v("rs" + s, t, t + 1))
-        quant(v("cq" + s, 0, K), v("ct"))
-        mm(2, v("cq" + s, 128, 256), v("oneq"))
-        mm(1, v("cq" + s, 0, 128), v("oneq"))
-        tt(v("rf" + s, 1, 3), v("bs" + s, 1, 3), v("rs" + s, 1, 3), OP.add)
+            act(v("c0t", 8 * K + K * (t - 1), 8 * K + K * t), ct(t), AF.Copy, scale=-1.0, bias=6.0, accum=v("acc" + s, t, t + 1))
+        quant(v("cq" + s, 0, K), v("c0t", 0, 4 * K))
+        for t in range(2):
+            mm(t, v("cq" + s, 128 * t, 128 * t + 128), v("ftq" + s))
+        return here
 
-    def place(s, row, places):
-        for t in range(3):
-            ts(v("st", t, 4 * K, 4), v(row), *places[t])
-        quant(v("sq" + s, 64, 256), v("st"))
+    ts(v("off0"), listof(6, "nrep", v("oh"), "sc0"), v("cn"), OP.add)
+    give("0", rank ^ 1, "q0", send(rank ^ 1, v("ofb0"), v("off0"), "ls0"))
+    arrive("ls0")
+    before("0", "q0")
+    scatter(v("inv0"), v("ofb0"), v("val0"))
+    for a in range(0, P, K):
+        n = min(K, P - a)
+        scan(v("scy", a, a + n), v("lk", 0, n), v("inv0", a, a + n))
+    ts(v("offy"), v("scy", 15, P, 16), -512.0, OP.mult, v("cy"), OP.add)
+    ts(v("hi"), v("nnc0"), ROUND16, OP.add, -ROUND16, OP.add)
+    tt(v("lo"), v("nnc0"), v("hi"), OP.subtract)
+    for t in range(3):
+        act(v("nrept", t, 512, 4), one, AF.Identity, scale=v("hi", t, t + 1))
+        act(v("nrept", 512 + t, 1024, 4), one, AF.Identity, scale=v("lo", t, t + 1))
+    quant(v("drq"), v("nrept"))
+    merge("0")
+    for a in range(0, P, 256):
+        pick(v("dy", a, a + 256), v("win0"), v("offy", a // 16, (a + 256) // 16))
 
-    def chosen(s, out):
-        listof(6, (v("dhq" + s), v("dlq")), v("sq" + s, 64, 256), v("scs" + s), v("offs" + s), v("cw"))
-        pick(out, v("win" + s), v("offs" + s))
+    ts(high(st(1)), high(v("i192")), high(ps(2, 0, 1)), OP.subtract, high(v("acc0", 1, 2)), OP.is_equal)
+    ts(st(2), v("i192"), ps(3, 0, 1), OP.subtract, v("acc0", 2, 3), OP.is_equal)
+    ts(st(0), v("i192"), ps(0, 0, 1), OP.is_equal)
+    ts(low(st(1)), low(v("i192")), low(ps(1, 0, 1)), OP.is_equal)
+    quant(v("sq0"), v("ot"))
+    last = listof(6, "drq", v("sq0"), "sc1")
+    ts(low(v("msg")), low(v("sc1", 15, K // 2, 16)), -1.0, OP.mult, low(v("cm")), OP.add)
+    ts(high(v("msg")), high(v("sc1", K // 2 + 15, K, 16)), -1.0, OP.mult, high(v("cm")), OP.add)
+    ts(v("off1"), last, -1.0, OP.mult, v("cm"), OP.add)
+    give("1", rank ^ 2, "dy", send(rank ^ 2, v("lnd"), v("msg"), "ls1"))
 
-    def weigh(a, banks):
+    def weigh(x, a, banks):
         for o in range(O):
-            mm(banks[o], v("wq", 128 * o, 128 * o + 128), v("win1", a, a + K))
+            mm(banks[o], v("wq", 128 * o, 128 * o + 128), x)
             act(v("yw%d" % o, a, a + K), ps(banks[o], 0, K), AF.Copy)
 
-    mark = describe("0", rank ^ 1, "oh", "ndcq")
-    listof(6, (v("nrep", 0, 128), v("nrep", 128, 256)), v("oh", 64, 256), v("sc"), v("off0"), v("cn"))
-    act(v("nr0", 0, K), ps(6, 0, K), AF.Copy)
-    pick(v("win0", WA, WB), v("q0"), v("off0"))
-    sendmx(rank ^ 1, v("win0", WB, WZ), v("win0", WA, WB), "wc0", "ws0")
-    for s in "01":
-        after = early[3] if s == "0" else mark
-        mxcopy("y", v("tl" + s, 8, 128), v("zq", 0, 120), [after])
-        mxcopy("y", v("mtq" + s, K, 256), v("zq", 0, 256 - K), [after])
-        mxcopy("y", v("cq" + s, K, 256), v("zq", 0, 256 - K), [after])
-        mxcopy("y", v("win" + s, 0, WA), v("zq", 0, WA), [after])
-        mxcopy("y", v("win" + s, WZ, WM), v("zq", 0, WM - WZ), [after])
-        mxcopy("y", v("win" + s, WY, WE), v("zq", 0, WE - WY), [after])
-    dma("y", v("wt"), lambda: T.w[:, :], [], [v("wt")], [mark])
-    act(v("urt", 16, 20), v("ut"), AF.Copy)
-    quant(v("uq"), v("urt", 0, 544))
-    quant(v("triq"), v("trit"))
-    quant(v("dlq"), v("dlt"))
-    own("0")
-    before("0", False)
-    merge("0")
+    weigh(v("win1", WA, WA + K), K, (5, 7))
+    arrive("ls1")
+    for h, half in enumerate((low, high)):
+        for to in (low, high):
+            cp(to(v("ofb1", 6 * h, 6 * h + 6)), half(v("lnd")))
+    before("1", "dy")
+    ts(v("offc"), v("scv1", 15, K, 16), -512.0, OP.mult, v("cy"), OP.add)
+    for t in range(3):
+        act(orda(t), v("nr1", K, 2 * K), AF.Sign, bias=v("nnc1", t, t + 1))
+    quant(v("cq1", 2 * K, 3 * K), v("junk", 0, 4 * K))
+    ts(v("nd", 0, 3), v("nnc1"), ROUND16, OP.add, -ROUND16, OP.add)
+    tt(v("nd", 8, 11), v("nnc1"), v("nd", 0, 3), OP.subtract)
+    quant(v("ndq"), v("nd"))
+    here = merge("1")
+    mxcopy("y", v("fw", K, 2 * K), v("win1", WA, WA + K), here)
+    pick(v("fw", 0, K), v("win1"), v("offc"))
+    weigh(v("fw", 0, K), 0, (7, 7))
 
-    place("0", "i192", ((ps(1, 0, 1), OP.is_equal), (ps(2, 0, 1), OP.subtract, v("rf0", 1, 2), OP.is_equal), (v("rf0", 2, 3), OP.is_equal)))
-    describe("1", rank ^ 2, "sq0", "ndq0")
-    chosen("0", v("win1", WA, WB))
-    sendmx(rank ^ 2, v("win1", WB, WZ), v("win1", WA, WB), "wc1", "ws1")
-    quant(v("wq"), v("wt"))
-    own("1")
-    weigh(WA, (5, 6))
-    before("1", True)
-    merge("1")
-    weigh(WB, (3, 7))
-    weigh(WM, (3, 7))
-
-    ts(v("plc"), v("rf1"), -1.0, OP.mult, K - 0.5, OP.add)
-    ts(mi("xt", 2, 3), v("plc", 2, 3), 0.0, OP.is_gt)
-    tt(mi("xt", 0, 2), pst(1, 2, 0), v("plc", 0, 2), OP.is_lt)
-    quant(v("xq"), mi("xt", 0, 512))
-    ts(v("ntk"), mi("xt", 0, 3), -1024.0, OP.mult, 1024.0, OP.add)
-    for c in range(3):
-        mm(c, v("ordq", 128 * c, 128 * c + 128), v("xq"))
-    fin = v("fin")
-    place("1", "i2", [(ps(t, 0, 1), OP.subtract, v("ntk", t, t + 1), OP.is_equal) for t in range(3)])
-    chosen("1", fin)
-    for o in range(O):
-        gather("vs"[o], v("yb", K * o, K * o + K), v("yw%d" % o), v("offs1"))
-    mm(4, v("ndq1", 4, 132), v("sq1", 64, 256), True, False)
-    mm(4, v("ndq1", 6, 134), v("sq1", 64, 256), False, True)
-    ts(v("nbw", 0, K, 1, 0, 1), v("ps", 4 * 512, 4 * 512 + K, 1, 0, 1), 256.0, OP.add)
-    dma("y", lambda: T.nb[:, :], lambda: T.nbw[0:1, :], [v("nbw", 0, K, 1, 0, 1)], [])
-    dma("y", lambda: T.oc[:, :], lambda: T.fin[:, :].bitcast(dt.uint8), [fin], [])
+    ts(high(v("xt", 1, 2)), high(ps(2, 0, 1)), high(v("acc1", 1, 2)), OP.add, K - 0.5, OP.is_lt)
+    ts(v("xt", 2, 3), ps(3, 0, 1), v("acc1", 2, 3), OP.add, K - 0.5, OP.is_lt)
+    ts(v("xt", 0, 1), ps(0, 0, 1), K - 0.5, OP.is_lt)
+    ts(low(v("xt", 1, 2)), low(ps(1, 0, 1)), K - 0.5, OP.is_lt)
+    quant(v("xq"), v("xt"))
+    ts(v("ntk"), v("xt", 0, 3), -1024.0, OP.mult, 1024.0, OP.add)
+    for t in range(3):
+        mm(4 + t, v("cq1", K + 128 * t, K + 128 * t + 128), v("xq"))
+        ts(st(t), v("i2"), ps(4 + t, 0, 1), OP.subtract, v("ntk", t, t + 1), OP.is_equal)
+    quant(v("sq1"), v("ot"))
+    off2, fin = v("off2"), v("fin")
+    ts(off2, listof(0, "nrep", v("sq1"), "sc2"), v("cn"), OP.add)
+    pick(fin, v("fw"), off2)
+    gather(v("yb", 0, K), v("yw0"), off2)
+    act(v("yb", K, 2 * K), v("yw1"), AF.Copy, off=off2)
+    mm(1, v("ndq", 0, 128), v("sq1"), True, False)
+    mm(1, v("ndq", 2, 130), v("sq1"), False, True)
+    act(v("nbw", 0, K, 1, 0, 1), v("ps", 512, 512 + K, 1, 0, 1), AF.Copy, scale=-1.0, bias=256.0)
+    dma("y", lambda: T.nb[:, :], lambda: T.nbw[0:1, 0:K], [v("nbw", 0, K, 1, 0, 1)], [], store=True)
+    dma("y", lambda: T.oc[:, :], lambda: T.fin[:, 0:K].bitcast(dt.uint8), [fin], [], store=True)
     for k in range(4):
-        dma("sy"[k % 2], (lambda k=k: T.osc[4 * k:4 * k + 4, :]), (lambda k=k: T.fins[32 * k:32 * k + 4, :]), [pl(fin)], [])
-    dma("y", lambda: T.y[:, 0:K], v("yb", 0, K), [v("yb", 0, K)], [])
-    dma("s", lambda: T.y[:, K:2 * K], v("yb", K, 2 * K), [v("yb", K, 2 * K)], [])
+        dma("y", (lambda k=k: T.osc[4 * k:4 * k + 4, :]), (lambda k=k: T.fins[32 * k:32 * k + 4, 0:K]), [pl(fin)], [], store=True)
+    dma("y", lambda: T.y[:, 0:K], v("yb", 0, K), [v("yb", 0, K)], [], store=True)
+    dma("s", lambda: T.y[:, K:2 * K], v("yb", K, 2 * K), [v("yb", K, 2 * K)], [], store=True)
 
     acc, edges = {}, []
     for i, r in enumerate(prog):
-        e = {j: True for j in r["after"] if r["kind"] != "a"}
+        e = {j: r["q"] != prog[j]["q"] for j in r["after"] if r["kind"] != "a"}
         for regs, w in ((r["reads"], False), (r["writes"], True)):
             for x in regs:
                 for (y, yw, j) in acc.get(x[0], ()):
                     if j == i or not (w or yw or x[0] == "ps") or not overlap(x, y):
                         continue
                     if prog[j]["q"] == r["q"] and prog[j]["kind"] == "c" and r["kind"] == "c":
-                        wait = yw and not (r["q"] == "t" and x[0] == "ps")
+                        wait = (w or yw) and not (r["q"] == "t" and x[0] == "ps")
                     else:
                         wait = w or yw or x[0] == "ps"
                     if x[0] == "ps" and not w and not yw and prog[j]["q"] == r["q"]:
@@ -554,122 +489,9 @@ def rank_program(g, core, T, topo):
         for x in r["writes"]:
             acc.setdefault(x[0], []).append((x, True, i))
 
-    n = len(prog)
-    preds = [dict(e) for e in edges]
-    for i, r in enumerate(prog):
-        if r["kind"] == "a":
-            preds[i][r["after"][0]] = True
-    succ = [[] for _ in prog]
-    for i, e in enumerate(preds):
-        for j, wait in e.items():
-            succ[j].append((i, wait))
-
-    def guess(compute, product, wake, same, local, link, big):
-        cost = [r["cost"] * (product if r["q"] == "t" else 1.0 if r["kind"] != "c" else compute) for r in prog]
-        lag = {"c": 0.0, "d": local, "r": link, "a": 0.0}
-        gaps = [{j: (0.0 if not wait else lag[prog[j]["kind"]] + (same if prog[j]["q"] == prog[i]["q"] and prog[j]["kind"] == "c" else wake)) for j, wait in e.items()} for i, e in enumerate(preds)]
-        for i, r in enumerate(prog):
-            if r["kind"] == "a" and r["sem"][2] == "w":
-                gaps[i][r["after"][0]] += big
-        return cost, lag, gaps, cost, [lag[r["kind"]] for r in prog], [[(j, d) for j, d in e.items() if d] for e in gaps]
-
-    qn = {q: k for k, q in enumerate("vstgy")}
-    queue = [qn.get(r["q"], 5) for r in prog]
-
-    def length(order, model):
-        cost, lag, gaps = model[3:]
-        end, free, top = [0.0] * n, [0.0] * 6, 0.0
-        for i in order:
-            q = queue[i]
-            x = free[q] if q < 5 else 0.0
-            for j, d in gaps[i]:
-                y = end[j] + d
-                if y > x:
-                    x = y
-            x += cost[i]
-            end[i] = free[q] = x
-            if x + lag[i] > top:
-                top = x + lag[i]
-        return top
-
-    def total(order):
-        return sum([length(order, m) / b for m, b in zip(models, BASE)])
-
-    def arrange(model, weight, margin, soon):
-        cost, lag, gaps = model[:3]
-        tail = [0.0] * n
-        for j in range(n - 1, -1, -1):
-            tail[j] = max([tail[i] + gaps[i][j] for i, wait in succ[j]] + [lag[prog[j]["kind"]]]) + cost[j]
-        urge = [t * w for t, w in zip(tail, weight)]
-        left, ready, end, free, order = [len(e) for e in preds], {}, [0.0] * n, {}, []
-        for i in range(n):
-            if not left[i]:
-                ready.setdefault(prog[i]["q"], {})[i] = 0.0
-        for _ in range(n):
-            best = None
-            for q, calls in ready.items():
-                if not calls:
-                    continue
-                f = free.get(q, 0.0) if q else 0.0
-                top = max(urge[i] for i in calls)
-                c = [(max(f, t + (margin if urge[i] < top - 1500.0 else 0.0)), -urge[i], i) for i, t in calls.items()]
-                first = min(c)[0]
-                for x in sorted((x for x in c if x[0] <= first + soon), key=lambda x: x[1]):
-                    e = x[0] + cost[x[2]]
-                    if not any(y[0] < e - soon and y[1] < x[1] - 300.0 for y in c):
-                        break
-                else:
-                    x = min((y for y in c if y[0] <= first + soon), key=lambda y: y[1])
-                if best is None or x < best:
-                    best = x
-            i = best[2]
-            q = prog[i]["q"]
-            t = ready[q].pop(i)
-            end[i] = max(t, free.get(q, 0.0) if q else 0.0) + cost[i]
-            free[q] = end[i]
-            order.append(i)
-            for k, wait in succ[i]:
-                left[k] -= 1
-                if not left[k]:
-                    ready.setdefault(prog[k]["q"], {})[k] = max(end[j] + d if d else end[j] - cost[j] for j, d in gaps[k].items())
-        return order
-
-    if "order" not in ORDER:
-        models = [guess(*x) for x in GUESSES]
-        state, found = 1, None
-        for trial in range(TRIALS):
-            weight = []
-            for i in range(n):
-                state = (state * 1103515245 + 12345) % 2 ** 31
-                weight.append(1.0 + (state / 2.0 ** 31 - 0.5) * (0.0, 0.02, 0.05, 0.1)[trial % 4])
-            o = arrange(models[trial % len(models)], weight, (0.0, 80.0, 160.0, 240.0, 320.0)[trial % 5], (30.0, 60.0, 100.0)[trial % 3])
-            t = total(o)
-            if found is None or t < found[0]:
-                found = (t, o)
-        t, order = found
-        state, place = 7, {i: k for k, i in enumerate(order)}
-        for trial in range(MOVES):
-            state = (state * 1103515245 + 12345) % 2 ** 31
-            a = (state >> 8) % n
-            i = order[a]
-            lo = max([place[j] + 1 for j in preds[i]] + [a - 60, 0])
-            hi = min([place[k] - 1 for k, _ in succ[i]] + [a + 60, n - 1])
-            state = (state * 1103515245 + 12345) % 2 ** 31
-            b = lo + (state >> 8) % (hi - lo + 1)
-            if a == b:
-                continue
-            o = list(order)
-            o.pop(a)
-            o.insert(b, i)
-            t2 = total(o)
-            if t2 <= t:
-                t, order = t2, o
-                for k in range(min(a, b), max(a, b) + 1):
-                    place[o[k]] = k
-        ORDER["order"] = order
-        ORDER["found"] = t
-    order = ORDER["order"]
+    order = list(ORDER)
     place = {i: k for k, i in enumerate(order)}
+    assert sorted(order) == list(range(len(prog))) and all(place[j] < place[i] for i, e in enumerate(edges) for j in e)
     deps = [sorted(place[j] for j, wait in edges[i].items() if wait) for i in order]
     prog = [prog[i] for i in order]
 
@@ -693,9 +515,7 @@ def rank_program(g, core, T, topo):
         s[key(i)[0]] = key(i)[1]
         snap.append(s)
         need.append(ds)
-    lastc = {r["q"]: i for i, r in enumerate(prog) if r["kind"] == "c"}
-    used |= set(lastc.values())
-    total, val = {q: 0 for q in lastc}, {}
+    total, val, waited = {q: 0 for q in "vstg"}, {}, set()
     for i, r in enumerate(prog):
         if r["q"] is None:
             continue
@@ -706,6 +526,7 @@ def rank_program(g, core, T, topo):
                 e.wait_ge(T.sem["q_" + p["q"]], val[d])
             else:
                 e.wait_ge(T.sem[p["sem"]], p["amount"])
+                waited.add(d)
         ins = r["fn"]()
         if r["kind"] == "c" and i in used:
             total[r["q"]] += 1
@@ -713,8 +534,7 @@ def rank_program(g, core, T, topo):
             ins.then_inc(T.sem["q_" + r["q"]], 1)
         elif r["kind"] == "d":
             ins.then_inc(T.sem[r["sem"]], 16)
-    for q in total:
-        g.wait_ge(T.sem["q_" + q], total[q])
-    for r in prog:
-        if r["kind"] in "dra":
+    for i, r in enumerate(prog):
+        if r["kind"] in "dra" and r["sem"] != "out" and i not in waited:
             g.wait_ge(T.sem[r["sem"]], r["amount"])
+    g.wait_ge(T.sem["out"], sum(16 for r in prog if r["sem"] == "out"))

from concourse.mybir import dt, AluOpType as OP, ActivationFunctionType as AF

P, K, O = 512, 192, 2
WM, WZ, WA, WB, WE = 0, 192, 256, 512, 704
ZB = 224
NSEM = 24
LIFT = 1024.0
ROUND16 = 1.5 * 2.0 ** 27
ROUND2 = 1.5 * 2.0 ** 24
BF, F32, I32, U16, CODE, U8 = "bfloat16", "float32", "int32", "uint16", "float8_e4m3fn_x4", "uint8"
SCRATCH = {"ps": ("psum", [128, 4096], F32)}
PLACE = {}
_TOP = {}
_ALIGN = {BF: 16, F32: 8, I32: 8, U16: 16}
_ALONE = ("ut", "urt", "grt", "wt", "nbw", "yb", "yw0", "yw1", "kz", "ofb0", "ofb1", "off0", "off1", "msg", "lnd", "trit", "mem1")
_CONST = []
ORDER = (
    1, 0, 2, 15, 12, 9, 10, 6, 5, 7, 14, 20, 41, 16, 21, 17, 51, 19, 13, 11, 23, 47, 40, 3, 4, 36, 48, 49, 46, 18, 35, 33, 34, 32, 50, 53, 52, 22, 26, 8, 56, 61, 124, 55, 54, 58, 57,
    27, 60, 59, 66, 63, 62, 71, 68, 67, 65, 64, 39, 73, 79, 75, 78, 76, 38, 70, 83, 82, 84, 72, 69, 74, 93, 80, 81, 77, 30, 92, 87, 88, 99, 98, 94, 100, 85, 101, 86, 102, 91, 95, 96,
    89, 97, 103, 90, 122, 119, 121, 120, 123, 24, 112, 25, 126, 127, 107, 110, 105, 104, 111, 106, 113, 42, 128, 129, 45, 44, 131, 136, 118, 31, 135, 138, 43, 116, 132, 114, 130, 133,
    134, 139, 115, 28, 140, 137, 182, 181, 141, 109, 108, 117, 29, 143, 149, 148, 150, 142, 146, 147, 145, 144, 151, 167, 152, 153, 154, 185, 187, 189, 183, 155, 37, 184, 125, 156,
    157, 158, 186, 191, 188, 190, 192, 172, 197, 193, 195, 194, 196, 169, 159, 163, 160, 161, 170, 173, 168, 162, 198, 199, 200, 176, 174, 203, 204, 166, 165, 205, 207, 164, 201, 202,
    209, 178, 179, 177, 175, 206, 208, 210, 211, 212, 171, 213, 180, 214, 215, 221, 220, 222, 223, 224, 216, 225, 226, 227, 230, 229, 228, 218, 232, 217, 219, 236, 233, 243, 241, 239,
    231, 237, 235, 234, 284, 283, 245, 246, 247, 248, 249, 240, 251, 250, 258, 259, 238, 257, 253, 255, 254, 252, 260, 262, 261, 319, 318, 285, 287, 289, 291, 293, 244, 256, 288, 290,
    263, 286, 265, 278, 264, 266, 276, 242, 292, 294, 297, 298, 295, 296, 280, 299, 300, 267, 271, 275, 268, 269, 320, 277, 279, 270, 301, 302, 305, 274, 273, 306, 307, 272, 303, 304,
    309, 311, 308, 310, 312, 281, 315, 313, 314, 321, 316, 317, 322, 323, 282, 327, 326, 328, 329, 330, 331, 332, 334, 336, 324, 333, 335, 337, 338, 339, 340, 347, 348, 325, 341, 342,
    343, 345, 349, 344, 346, 350, 351, 357, 353, 352, 356, 354, 355)


def _buf(name, n, t):
    assert name not in PLACE, name
    if t in _ALIGN and name not in _ALONE:
        home = ("k" if name in _CONST else "m") + t
        top = _TOP.get(home, 0)
        PLACE[name] = (home, top, n)
        _TOP[home] = -(-(top + n) // _ALIGN[t]) * _ALIGN[t]
        SCRATCH[home] = ("sbuf", [128, _TOP[home]], t)
    else:
        SCRATCH[name] = ("sbuf", [128, n], t)
        PLACE[name] = (name, 0, n)


def _mx(name, n):
    _buf(name, n, CODE)
    _buf(name + "s", n, U8)


for _n, _w, _t in (
        ("i16", K, BF), ("i192", K, BF), ("i2", K, BF), ("i512", P, BF), ("ebf", 515, BF), ("upp", 128, BF), ("tri0", 128, BF), ("trit", 1024, BF),
        ("lk", K, BF), ("dg", 128, BF), ("ni", 1, I32), ("nl", 1, I32), ("nf", 4, F32), ("nlf", 1, F32), ("nx", 4, F32), ("b511", 4, F32),
        ("vala", K, F32), ("valb", K, F32), ("cn", 1, F32), ("cm", 1, F32), ("cy", 1, F32), ("cb", 1, F32), ("cd", 1, F32)):
    _CONST.append(_n)
    _buf(_n, _w, _t)
for _n, _w, _t in (
        ("kz", 744, BF), ("ut", 4, BF), ("urt", 512, BF), ("grt", 4 * P, BF), ("wt", 1024, BF), ("nrept", 1024, BF),
        ("srow", P, F32), ("scol", 4, F32), ("xd", 512, BF), ("c0t", 4 * P, BF), ("p0", 16, F32), ("junk", 10 * 128, BF),
        ("x1", 4, F32), ("x2", 4, F32), ("x3", 4, F32), ("ot", 4 * K, BF), ("inv0", P, F32), ("mem0", P, BF), ("mem1", P, BF), ("scy", P, F32), ("offy", 32, U16),
        ("hi", 3, F32), ("lo", 3, F32), ("msg", 6, U16), ("lnd", 6, U16), ("offc", 12, U16), ("off2", 12, U16), ("sc2", K, F32),
        ("ntk", 3, F32), ("nbw", K, F32), ("yb", O * K, F32), ("yw0", 2 * K, F32), ("yw1", 2 * K, F32)):
    _buf(_n, _w, _t)
for _n, _a, _w in (("nd", 0, 520), ("ft1", 12, 512), ("ft0", 16, 512), ("one", 20, 512), ("xt", 212, 512), ("zt", 216, 528)):
    PLACE[_n] = ("kz", _a, _w)
for _n, _w in (("ur", 128), ("q0", P), ("wq", 256), ("oneq", 128), ("nrep", 256), ("eq", 512), ("triq", 256), ("c0q", P), ("oh", K),
               ("drq", 256), ("dy", P), ("ndq", 130), ("xq", 128), ("fw", 2 * K), ("fin", K)):
    _mx(_n, _w)
for _s in "01":
    for _n, _w, _t in (
            ("sc", K, F32), ("off", 12, U16), ("ofb", 12, U16), ("nr", 2 * K, BF), ("bor", K, BF), ("val", K, F32), ("scv", K, F32), ("offn", 12, U16),
            ("scd", 2 * K, F32), ("nnc", 3, F32), ("par", 3, F32), ("even", 3, F32), ("ht", 4 * K, BF), ("arow", K, F32), ("acol", 3, F32), ("v", 3 * K, BF), ("acc", 3, F32)):
        _buf(_n + _s, _w, _t)
    for _n, _w in (("win", WE), ("ap", K), ("bn", 256), ("ftq", 128), ("cq", 2 * K if _s == "0" else 3 * K), ("sq", K)):
        _mx(_n + _s, _w)
ARR = ["ls0", "wc0", "ws0", "ls1", "wc1", "ws1"]
SEMAPHORES = ["q_v", "q_s", "q_t", "q_g", "out"] + ["d%d" % i for i in range(NSEM)] + ["l_" + a for a in ARR] + ["a_" + a for a in ARR]


def rank_program(g, core, T, topo):
    rank = T.rank_of(core)
    if rank is None:
        return
    ENG = {"v": g.vector, "s": g.scalar, "t": g.tensor, "g": g, "y": g.sync}
    prog, nd, sent = [], [0], {}

    def v(name, a=0, b=None, s=1, p=0, e=128, cast=None):
        if name == "ps":
            return (name, a, b, s, p, e, cast)
        home, o, n = PLACE[name]
        return (home, o + a, o + (n if b is None else b), s, p, e, cast)

    low = lambda x: x[:4] + (0, 64) + x[6:]
    high = lambda x: x[:4] + (64, 128) + x[6:]

    def ap(x):
        if not isinstance(x, tuple):
            return x
        name, a, b, s, p, e, cast = x
        t = T[name]
        r = t[p:e, a:b] if s == 1 else t[p:e, a:b:s]
        if cast is None:
            return r
        return r.bitcast(dt.uint8 if cast == 8 else dt.uint32)

    def width(x):
        return len(range(x[1], x[2], x[3]))

    def overlap(x, y):
        if x[0] == "ps":
            f = lambda r: set(c // 512 for c in range(r[1], r[2], r[3] if r[3] == 512 else 1))
            return bool(f(x) & f(y))
        if x[1] >= y[2] or y[1] >= x[2] or x[4] >= y[5] or y[4] >= x[5]:
            return False
        if x[3] == y[3] and x[3] > 1:
            return (x[1] - y[1]) % x[3] == 0
        return True

    def rec(q, fn, reads, writes, kind="c", sem=None, amount=0, after=()):
        prog.append({"q": q, "fn": fn, "reads": reads, "writes": writes, "kind": kind, "sem": sem, "amount": amount, "after": list(after)})
        return len(prog) - 1

    tens = lambda *xs: [x for x in xs if isinstance(x, tuple)]

    def ts(out, in0, s1, op0, s2=None, op1=None):
        if op1 is None:
            fn = lambda: g.vector.tensor_scalar(out=ap(out), in0=ap(in0), scalar1=ap(s1), scalar2=None, op0=op0)
        else:
            fn = lambda: g.vector.tensor_scalar(out=ap(out), in0=ap(in0), scalar1=ap(s1), scalar2=ap(s2), op0=op0, op1=op1)
        return rec("v", fn, tens(in0, s1, s2), [out])

    def tt(out, a, b, op, off=None):
        rec("v", lambda: g.vector.tensor_tensor(out=ap(out), in0=ap(a).indirect(ap(off)) if off else ap(a), in1=ap(b), op=op), tens(a, b, off), [out])

    def cp(out, a):
        rec("v", lambda: g.vector.tensor_copy(ap(out), ap(a)), [a], [out])

    def fill(out, c=0.0):
        rec("v", lambda: g.vector.memset(ap(out), c), [], [out])

    def scan(out, lift, row):
        rec("v", lambda: g.vector.tensor_tensor_scan(ap(out), ap(lift), ap(row), 0.0, OP.add, OP.max), [lift, row], [out])

    def act(out, a, func, bias=None, scale=None, accum=None, off=None):
        kw = {k: x for k, x in (("bias", bias), ("scale", scale), ("accum_out", accum)) if x is not None}
        rec("s", lambda: g.scalar.activation(ap(out), ap(a).indirect(ap(off)) if off else ap(a), func, **{k: ap(x) for k, x in kw.items()}), tens(a, bias, scale, off), tens(out, accum))

    def zero(out):
        act(out, v("zt", 0, width(out)), AF.Copy)

    def pl(x):
        return (x[0] + "s",) + x[1:6] + (None,)

    def quant(out, a, after=()):
        return rec("v", lambda: g.vector.quantize_mx(ap(out), ap(pl(out)), ap(a)), [a], [out, pl(out)], after=after)

    def mm(bank, l, r, start=True, stop=True):
        out = v("ps", 512 * bank, 512 * bank + width(r))
        rec("t", lambda: g.tensor.matmul_mx(ap(out), ap(l), ap(pl(l)), ap(r), ap(pl(r)), start, stop), [l, pl(l), r, pl(r)], [out])

    def gather(out, win, off, c=lambda x: x):
        rec("v", lambda: g.vector.tensor_copy(ap(c(out)), ap(c(win)).indirect(ap(off))), [win, off], [out])

    def scatter(win, off, a):
        rec("v", lambda: g.vector.tensor_copy(ap(win).indirect(ap(off)), ap(a)), [a, off, win], [win])

    def pick(out, win, off):
        gather(out, win, off, lambda x: x[:6] + (32,))
        act(pl(out), pl(win), AF.Copy, off=off)

    def dma(q, out, in_, reads, writes, after=(), store=False):
        sem = "out" if store else "d%d" % nd[0]
        nd[0] += not store
        rec(q, lambda: ENG[q].dma_start(out() if not isinstance(out, tuple) else ap(out), in_() if not isinstance(in_, tuple) else ap(in_)), reads, writes, "d", sem, 16, after)

    def mxcopy(q, out, in_, after=()):
        c = lambda x: x[:6] + (8,)
        dma(q, c(out), c(in_), [in_], [out], after)
        dma(q, pl(out), pl(in_), [pl(in_)], [pl(out)], after)

    def send(peer, out, in_, key, after=()):
        dst = T.cores[peer]
        rid, pid, _ = topo.addr(dst)
        m, n = topo.mask(core, dst), len(topo.engines(core, dst))
        i = rec("g", lambda: g.remote_dma(ap(out), ap(in_), T.sem["a_" + key], T.sem["l_" + key], pid, rid, m), [in_], [], "r", "l_" + key, n, after)
        sent[key] = (i, out, len(topo.engines(dst, core)))
        return i

    def sendmx(peer, out, in_, kc, ks, after=()):
        c = lambda x: x[:6] + (8,)
        send(peer, c(out), c(in_), kc, after)
        send(peer, pl(out), pl(in_), ks, after)

    def arrive(key):
        i, out, n = sent[key]
        return rec(None, None, [], [out], "a", "a_" + key, n, [i])

    ps = lambda bank, a, b, s=1: v("ps", 512 * bank + a, 512 * bank + b, s)
    pst = lambda bank, n, c: v("ps", 512 * bank + c, 512 * (bank + n - 1) + c + 1, 512)
    one = v("one", 0, 128)
    eb = lambda b: v("eq", 128 * b, 128 * b + 128)

    def iota(out, pattern, base, cm, flag=True):
        kw = {"allow_small_or_imprecise_dtypes": True} if flag else {}
        rec("g", lambda: g.iota(ap(out), pattern, base, cm, **kw), [], [out])

    def select(out, in_, pattern, op, fillv, base, cm):
        rec("g", lambda: g.affine_select(ap(out), ap(in_), pattern, op, fillv, base, cm), [in_], [out])

    dma("y", v("ut"), lambda: T.u[:, 0:4], [], [v("ut")])
    for c in range(4):
        x = v("grt", 512 * c, 512 * c + 512)
        dma("sy"[c % 2], x, (lambda c=c: T.gr[:, 512 * c:512 * c + 512]), [], [x])

    fill(v("kz", 0, 212), 1.0)
    fill(v("kz", 212, 744))
    select(v("upp"), one, [[1, 128]], OP.is_gt, 0.0, 0, -1)
    ts(v("tri0"), v("upp"), -1.0, OP.mult, 0.5, OP.add)
    iota(v("ni"), [[0, 1]], 0, 1, False)
    iota(v("nf"), [[128, 4]], -256, 1)
    iota(v("b511"), [[-128, 4]], 511, -1)
    iota(v("i16"), [[0, 12], [1, 16]], 0, 0)
    iota(v("i192"), [[1, K]], 0, 0)
    iota(v("i512"), [[1, P]], -256, 0)
    iota(v("cd"), [[0, 1]], 127 * int(LIFT), -int(LIFT))
    ts(v("nl"), v("ni"), 15, OP.bitwise_and)
    cp(v("nlf"), v("nl"))
    nlf = v("nlf")
    ts(v("nx"), v("nf"), nlf, OP.subtract)
    for t in (1, 2, 3):
        fill(v("c0t", t, 512 * t, 4))
    fill(v("p0"))
    quant(v("oneq"), v("one"))
    ts(v("lk"), v("i16"), nlf, OP.is_equal, -1.0e6, OP.mult)
    act(v("lk"), v("lk"), AF.Copy, bias=LIFT)
    lift = lambda out, c, f: act(out, nlf, AF.Copy, scale=LIFT * f, bias=c - LIFT * 15 * f)
    lift(v("cn"), 256.0, 1.0)
    lift(v("cm"), 256.0, -1.0)
    lift(v("cy"), 0.0, -512.0)
    lift(v("cb"), -float(ZB), -512.0)
    select(v("ebf"), v("zt", 0, 515), [[1, 515]], OP.not_equal, -0.5, -3, -4)
    ts(v("dg"), v("ebf", 3, 515, 4), 2.0e6, OP.mult, LIFT, OP.add)
    for t in range(4):
        act(v("nrept", t, 512, 4), one, AF.Identity, scale=v("nx", t, t + 1))
    act(v("nrept", 512, 1024), v("zt", 0, 512), AF.Identity, bias=nlf)
    act(v("i2"), v("i192"), AF.Copy, scale=2.0, bias=1.0 - K)
    act(v("vala"), v("i192"), AF.Copy, scale=-1.0 / 512, bias=-WA / 512.0)
    act(v("valb"), v("i192"), AF.Copy, scale=1.0 / 512, bias=WB / 512.0)
    zero(v("inv0"))
    zeros = quant(v("win0", 128, 256), v("zt", 0, 512))
    for b in range(4):
        quant(eb(b), v("ebf", 3 - b, 515 - b))

    for t in range(4):
        if t < 2:
            ts(v("urt", t, 512, 4), one, v("ut", t, t + 1), OP.mult)
        else:
            act(v("urt", t, 512, 4), v("zt", 0, 128), AF.Identity, bias=v("ut", t, t + 1))
    quant(v("ur"), v("urt"))
    ur = v("ur")

    def sizes(c):
        qc = v("q0", 128 * c, 128 * c + 128)
        i = quant(qc, v("grt", 512 * c, 512 * c + 512), [zeros] if c == 3 else [])
        mm(4 + c % 3, qc, ur)
        mm(c, ur, qc)
        act(v("scol", c, c + 1), ps(4 + c % 3, 0, 1), AF.Abs)
        act(v("srow", 128 * c, 128 * c + 128), ps(c, 0, 128), AF.Abs)
        return i

    def compare(c):
        for t in [c] + list(range(c)):
            blk = v("c0t", 512 * c + t, 512 * c + 512, 4)
            row = v("srow", 128 * c, 128 * c + 128)
            x = v("xd", 128 * c, 128 * c + 128)
            if t == c == 3:
                act(x, row, AF.Sign, bias=v("scol", c, c + 1), scale=-1.0)
                tt(blk, x, v("tri0"), OP.is_gt)
            elif t == c:
                ts(x, row, v("scol", t, t + 1), OP.is_le)
                select(blk, x, [[1, 128]], OP.is_gt, 0.0, 0, -1)
            else:
                ts(blk, row, v("scol", t, t + 1), OP.is_le)

    def count(c):
        for t in range(min(c + 1, 3)) if c else ():
            k = c * (c + 1) // 2 + t
            d = 128 if k == 1 else 0
            act(v("junk", 128 * k - d, 128 * k + 128), v("c0t", 512 * c + t - 4 * d, 512 * c + 512, 4), AF.Copy, accum=v("p0", 4 * c + t, 4 * c + t + 1))
        quant(v("c0q", 128 * c, 128 * c + 128), v("c0t", 512 * c, 512 * c + 512))
        mm(c, v("c0q", 128 * c, 128 * c + 128), v("oneq"))
        if c:
            tt(v("x%d" % c), v("b511") if c == 1 else v("x%d" % (c - 1)), v("p0", 4 * c, 4 * c + 4), OP.subtract)

    early = [sizes(c) for c in range(4)]
    for c in range(4):
        compare(c)
    for c in range(4):
        count(c)
    dma("y", v("wt"), lambda: T.w[:, :], [], [v("wt")], [early[3]])
    for name in ("win1", "bn0", "bn1"):
        mxcopy("y", v(name, WZ, WA), v("win0", WZ, WA), [early[3]])
    for x in (v("trit", 0, 512), v("trit", 512, 1024), v("mem1")):
        dma("y", x, v("zt", 0, 512), [v("zt", 0, 512)], [x], [early[3]])
    select(v("trit", 514, 1024, 4), v("upp"), [[1, 128]], OP.not_equal, -960.0, 0, -1)
    act(high(v("trit", 1, 512, 4)), high(v("trit", 514, 1024, 4)), AF.Copy)
    act(high(v("trit", 513, 1024, 4)), high(one), AF.Copy)
    quant(v("triq"), v("trit"))
    quant(v("wq"), v("wt"))

    def listof(bank, digits, onehot, sc):
        for k in range(2):
            mm(bank, v(digits, 128 * k, 128 * k + 128), onehot, k == 0, k == 1)
        scan(v(sc), v("lk"), ps(bank, 0, K))
        return v(sc, 15, K, 16)

    st = lambda t: v("ot", t, 4 * K, 4)
    for t in range(3):
        ts(st(t), v("i192"), ps(t, 0, 1), OP.subtract, v("x3", t, t + 1), OP.is_equal)
    ts(st(3), v("i192"), ps(3, 0, 1), OP.is_equal)
    quant(v("oh"), v("ot"))
    quant(v("nrep"), v("nrept"))
    zero(st(3))

    ct = lambda t: v("c0t", t, 4 * K, 4)
    ordb = lambda t: v("c0t", 4 * K + t, 8 * K, 4)
    orda = lambda t: v("junk", t, 4 * K, 4)

    def give(s, peer, table, first):
        w = "win" + s
        pick(v(w, WA, WA + K), v(table), v("off" + s))
        sendmx(peer, v(w, WB, WE), v(w, WA, WA + K), "wc" + s, "ws" + s, [first])
        act(v("nr" + s, K, 2 * K), ps(6, 0, K), AF.Copy, scale=-1.0 if s == "1" else 1.0)
        if s == "0":
            scatter(v("inv0"), v("off0"), v("vala"))
            act(v("mem0"), v("inv0"), AF.Sign, scale=-1.0)
        else:
            scatter(v("mem1"), v("off1"), v("one", 0, K))
        scan(v("scd" + s, 256, 384), v("dg"), v("nr" + s, 256, 384))
        mm(4, v(w, WA + 64, WA + K), ur)
        act(v("acol" + s, 2, 3), ps(4, 0, 1), AF.Abs)

    def before(s, table):
        ofb = v("ofb" + s)
        pick(v("ap" + s), v(table), ofb)
        for b in range(4):
            mm(b, eb(b), v("ap" + s), True, False)
        act(v("bor" + s), v("mem" + s), AF.Copy, scale=-2.0, off=ofb)
        act(v("nr" + s, 0, K), v("i512"), AF.Copy, off=ofb)
        tt(v("val" + s), v("mem" + s), v("valb"), OP.subtract, ofb)
        scan(v("scv" + s), v("lk"), v("val" + s))
        ts(v("offn" + s), v("scv" + s, 15, K, 16), -512.0, OP.mult, v("cb"), OP.add)
        for t in range(2):
            scan(v("scd" + s, 128 * t, 128 * t + 128), v("dg"), v("nr" + s, 128 * t, 128 * t + 128))
        act(v("nnc" + s), v("scd" + s, 127, 384, 128), AF.Identity, scale=-1.0, bias=v("cd"))
        for t in (1, 2, 0):
            act(ordb(t), v("nr" + s, 0, K), AF.Sign, bias=v("nnc" + s, t, t + 1), accum=v("par" + s, t, t + 1) if t else None)
        ts(v("even" + s, 1, 3), v("par" + s, 1, 3), ROUND2, OP.add, -ROUND2, OP.add)
        tt(high(v("ft" + s, 1, 2)), high(v("par" + s, 1, 2)), high(v("even" + s, 1, 2)), OP.is_equal)
        tt(v("ft" + s, 2, 3), v("par" + s, 2, 3), v("even" + s, 2, 3), OP.is_equal)
        quant(v("ftq" + s), v("ft" + s))
        quant(v("cq" + s, K, 2 * K), v("c0t", 4 * K, 8 * K))
        for t in range(3):
            mm(4 + t, eb(t), v("cq" + s, K, 2 * K))

    def merge(s):
        w, bn = "win" + s, "bn" + s
        here = [arrive("wc" + s), arrive("ws" + s)]
        pick(v(bn, 0, K), v(w, ZB, WE), v("offn" + s))
        for b in range(4):
            mm(b, eb(b), v(w, WB, WE), False, True)
            tt(v("ht" + s, b, 4 * K, 4), ps(b, 0, K), v("bor" + s), OP.mult)
        mm(7, ur, v(bn, 0, K), True, False)
        mm(0, v(bn, 0, 128), ur, True, False)
        mm(1, v(bn, 128, 256), ur, True, False)
        mm(1, v(w, WZ, WZ + 128), ur, False, False)
        quant(v(w, WM, WM + K), v("ht" + s))
        mm(7, ur, v(w, WM, WM + K), False, True)
        mm(0, v(w, WM, WM + 128), ur, False, True)
        mm(1, v(w, WM + 128, WM + 256), ur, False, True)
        for t in range(2):
            mm(2 + t, v("triq", 128 * t, 128 * t + 128), v("ftq" + s))
        act(v("arow" + s), ps(7, 0, K), AF.Abs)
        act(v("acol" + s, 0, 2), pst(0, 2, 0), AF.Abs)
        for t in (2, 1, 0):
            x = v("v" + s, K * t, K * t + K)
            act(x, v("arow" + s), AF.Sign, bias=v("acol" + s, t, t + 1), scale=-1.0)
            tt(ct(t), x, ps(4 + t, 0, K), OP.is_gt)
        for t in (2, 1):
            act(v("c0t", 8 * K + K * (t - 1), 8 * K + K * t), ct(t), AF.Copy, scale=-1.0, bias=6.0, accum=v("acc" + s, t, t + 1))
        quant(v("cq" + s, 0, K), v("c0t", 0, 4 * K))
        for t in range(2):
            mm(t, v("cq" + s, 128 * t, 128 * t + 128), v("ftq" + s))
        return here

    ts(v("off0"), listof(6, "nrep", v("oh"), "sc0"), v("cn"), OP.add)
    give("0", rank ^ 1, "q0", send(rank ^ 1, v("ofb0"), v("off0"), "ls0"))
    arrive("ls0")
    before("0", "q0")
    scatter(v("inv0"), v("ofb0"), v("val0"))
    for a in range(0, P, K):
        n = min(K, P - a)
        scan(v("scy", a, a + n), v("lk", 0, n), v("inv0", a, a + n))
    ts(v("offy"), v("scy", 15, P, 16), -512.0, OP.mult, v("cy"), OP.add)
    ts(v("hi"), v("nnc0"), ROUND16, OP.add, -ROUND16, OP.add)
    tt(v("lo"), v("nnc0"), v("hi"), OP.subtract)
    for t in range(3):
        act(v("nrept", t, 512, 4), one, AF.Identity, scale=v("hi", t, t + 1))
        act(v("nrept", 512 + t, 1024, 4), one, AF.Identity, scale=v("lo", t, t + 1))
    quant(v("drq"), v("nrept"))
    merge("0")
    for a in range(0, P, 256):
        pick(v("dy", a, a + 256), v("win0"), v("offy", a // 16, (a + 256) // 16))

    ts(high(st(1)), high(v("i192")), high(ps(2, 0, 1)), OP.subtract, high(v("acc0", 1, 2)), OP.is_equal)
    ts(st(2), v("i192"), ps(3, 0, 1), OP.subtract, v("acc0", 2, 3), OP.is_equal)
    ts(st(0), v("i192"), ps(0, 0, 1), OP.is_equal)
    ts(low(st(1)), low(v("i192")), low(ps(1, 0, 1)), OP.is_equal)
    quant(v("sq0"), v("ot"))
    last = listof(6, "drq", v("sq0"), "sc1")
    ts(low(v("msg")), low(v("sc1", 15, K // 2, 16)), -1.0, OP.mult, low(v("cm")), OP.add)
    ts(high(v("msg")), high(v("sc1", K // 2 + 15, K, 16)), -1.0, OP.mult, high(v("cm")), OP.add)
    ts(v("off1"), last, -1.0, OP.mult, v("cm"), OP.add)
    give("1", rank ^ 2, "dy", send(rank ^ 2, v("lnd"), v("msg"), "ls1"))

    def weigh(x, a, banks):
        for o in range(O):
            mm(banks[o], v("wq", 128 * o, 128 * o + 128), x)
            act(v("yw%d" % o, a, a + K), ps(banks[o], 0, K), AF.Copy)

    weigh(v("win1", WA, WA + K), K, (5, 7))
    arrive("ls1")
    for h, half in enumerate((low, high)):
        for to in (low, high):
            cp(to(v("ofb1", 6 * h, 6 * h + 6)), half(v("lnd")))
    before("1", "dy")
    ts(v("offc"), v("scv1", 15, K, 16), -512.0, OP.mult, v("cy"), OP.add)
    for t in range(3):
        act(orda(t), v("nr1", K, 2 * K), AF.Sign, bias=v("nnc1", t, t + 1))
    quant(v("cq1", 2 * K, 3 * K), v("junk", 0, 4 * K))
    ts(v("nd", 0, 3), v("nnc1"), ROUND16, OP.add, -ROUND16, OP.add)
    tt(v("nd", 8, 11), v("nnc1"), v("nd", 0, 3), OP.subtract)
    quant(v("ndq"), v("nd"))
    here = merge("1")
    mxcopy("y", v("fw", K, 2 * K), v("win1", WA, WA + K), here)
    pick(v("fw", 0, K), v("win1"), v("offc"))
    weigh(v("fw", 0, K), 0, (7, 7))

    ts(high(v("xt", 1, 2)), high(ps(2, 0, 1)), high(v("acc1", 1, 2)), OP.add, K - 0.5, OP.is_lt)
    ts(v("xt", 2, 3), ps(3, 0, 1), v("acc1", 2, 3), OP.add, K - 0.5, OP.is_lt)
    ts(v("xt", 0, 1), ps(0, 0, 1), K - 0.5, OP.is_lt)
    ts(low(v("xt", 1, 2)), low(ps(1, 0, 1)), K - 0.5, OP.is_lt)
    quant(v("xq"), v("xt"))
    ts(v("ntk"), v("xt", 0, 3), -1024.0, OP.mult, 1024.0, OP.add)
    for t in range(3):
        mm(4 + t, v("cq1", K + 128 * t, K + 128 * t + 128), v("xq"))
        ts(st(t), v("i2"), ps(4 + t, 0, 1), OP.subtract, v("ntk", t, t + 1), OP.is_equal)
    quant(v("sq1"), v("ot"))
    off2, fin = v("off2"), v("fin")
    ts(off2, listof(0, "nrep", v("sq1"), "sc2"), v("cn"), OP.add)
    pick(fin, v("fw"), off2)
    gather(v("yb", 0, K), v("yw0"), off2)
    act(v("yb", K, 2 * K), v("yw1"), AF.Copy, off=off2)
    mm(1, v("ndq", 0, 128), v("sq1"), True, False)
    mm(1, v("ndq", 2, 130), v("sq1"), False, True)
    act(v("nbw", 0, K, 1, 0, 1), v("ps", 512, 512 + K, 1, 0, 1), AF.Copy, scale=-1.0, bias=256.0)
    dma("y", lambda: T.nb[:, :], lambda: T.nbw[0:1, 0:K], [v("nbw", 0, K, 1, 0, 1)], [], store=True)
    dma("y", lambda: T.oc[:, :], lambda: T.fin[:, 0:K].bitcast(dt.uint8), [fin], [], store=True)
    for k in range(4):
        dma("y", (lambda k=k: T.osc[4 * k:4 * k + 4, :]), (lambda k=k: T.fins[32 * k:32 * k + 4, 0:K]), [pl(fin)], [], store=True)
    dma("y", lambda: T.y[:, 0:K], v("yb", 0, K), [v("yb", 0, K)], [], store=True)
    dma("s", lambda: T.y[:, K:2 * K], v("yb", K, 2 * K), [v("yb", K, 2 * K)], [], store=True)

    acc, edges = {}, []
    for i, r in enumerate(prog):
        e = {j: r["q"] != prog[j]["q"] for j in r["after"] if r["kind"] != "a"}
        for regs, w in ((r["reads"], False), (r["writes"], True)):
            for x in regs:
                for (y, yw, j) in acc.get(x[0], ()):
                    if j == i or not (w or yw or x[0] == "ps") or not overlap(x, y):
                        continue
                    if prog[j]["q"] == r["q"] and prog[j]["kind"] == "c" and r["kind"] == "c":
                        wait = (w or yw) and not (r["q"] == "t" and x[0] == "ps")
                    else:
                        wait = w or yw or x[0] == "ps"
                    if x[0] == "ps" and not w and not yw and prog[j]["q"] == r["q"]:
                        continue
                    e[j] = e.get(j, False) or wait
        edges.append(e)
        for x in r["reads"]:
            acc.setdefault(x[0], []).append((x, False, i))
        for x in r["writes"]:
            acc.setdefault(x[0], []).append((x, True, i))

    order = list(ORDER)
    place = {i: k for k, i in enumerate(order)}
    assert sorted(order) == list(range(len(prog))) and all(place[j] < place[i] for i, e in enumerate(edges) for j in e)
    deps = [sorted(place[j] for j, wait in edges[i].items() if wait) for i in order]
    prog = [prog[i] for i in order]

    know, snap, need, used = {}, [], [], set()
    key = lambda i: (prog[i]["q"], i) if prog[i]["kind"] == "c" else (i, 0)
    for i, r in enumerate(prog):
        k = know.setdefault(r["q"], {}) if r["q"] else {}
        last = {}
        for d in deps[i]:
            a, m = key(d)
            if k.get(a, -1) < m and (a not in last or key(last[a])[1] < m):
                last[a] = d
        ds = sorted(last.values())
        ds = [d for d in ds if not any(e != d and snap[e].get(key(d)[0], -1) >= key(d)[1] for e in ds)]
        for d in ds:
            used.add(d)
            for a, m in snap[d].items():
                if k.get(a, -1) < m:
                    k[a] = m
        s = dict(k)
        s[key(i)[0]] = key(i)[1]
        snap.append(s)
        need.append(ds)
    total, val, waited = {q: 0 for q in "vstg"}, {}, set()
    for i, r in enumerate(prog):
        if r["q"] is None:
            continue
        e = ENG[r["q"]]
        for d in need[i]:
            p = prog[d]
            if p["kind"] == "c":
                e.wait_ge(T.sem["q_" + p["q"]], val[d])
            else:
                e.wait_ge(T.sem[p["sem"]], p["amount"])
                waited.add(d)
        ins = r["fn"]()
        if r["kind"] == "c" and i in used:
            total[r["q"]] += 1
            val[i] = total[r["q"]]
            ins.then_inc(T.sem["q_" + r["q"]], 1)
        elif r["kind"] == "d":
            ins.then_inc(T.sem[r["sem"]], 16)
    for i, r in enumerate(prog):
        if r["kind"] in "dra" and r["sem"] != "out" and i not in waited:
            g.wait_ge(T.sem[r["sem"]], r["amount"])
    g.wait_ge(T.sem["out"], sum(16 for r in prog if r["sem"] == "out"))
